import numpy as np, ml_dtypes
CORES = [10,34,74,98]
N = 4
BF = ml_dtypes.bfloat16
def gentries(a):
    return np.ascontiguousarray(a.reshape(8, 16, -1).transpose(0, 2, 1)).reshape(8, -1)
def gtable(e):
    e = np.asarray(e); return np.ascontiguousarray(e.reshape(8, -1, 16).transpose(0, 2, 1)).reshape(128, -1).astype(np.int32)
W, NB, T, CA, LV, LI, LG = 4096, 4096, 6, 4, 8, 2, 2
P, S = NB // 16, W // (NB // 16)
def parts(rng):
    return rng.integers(0, 256, (N, 8, 16, W)), rng.integers(0, 256, (N, 8, 16, P)), rng.integers(0, 16, (N, 8, 16)), rng.integers(0, W, (N, 8, NB)), rng.integers(0, W, (N, 8, NB))
def pack(x, z, w, a, b):
    return {"xt": np.reshape(x, (N, 128, W)).astype(np.float32).astype(BF), "zp": np.reshape(z, (N, 128, P)).astype(np.float32).astype(BF), "wl": np.reshape(w, (N, 128, 1)).astype(np.float32).astype(BF),
            "ba": np.stack([gtable(v) for v in a]), "bb": np.stack([gtable(v) for v in b])}
def setup_inputs(rng):
    x, z, w, a, b = parts(rng)
    return pack(x, z, w, a, np.where(rng.random(b.shape) < 0.125, a, b))
def setup_inputs_corners(rng):
    x, z, w, a, b = parts(rng); pol = 255 * (np.arange(8) & 1)
    good = rng.random((N, 8, W)) < 0.5; good[..., W - 4:W - 1] = False
    far = np.abs(pol[None, :, None, None] - rng.integers(128, 256, x.shape))
    x = np.where(good[:, :, None, :], pol[None, :, None, None], far)
    z = np.broadcast_to(pol[None, :, None, None], z.shape).copy()
    o = np.argsort(rng.random((N, 8, 16)), axis=-1); v = rng.choice(np.array([128, 200]), (N, 8, 16))
    x[..., W - 4] = 128; x[..., W - 3] = np.where(o < LV, v, 60); x[..., W - 2] = np.where(o < LV - 1, v, 60)
    own = np.arange(NB).reshape(P, 16)
    for q in range(N):
        for g in range(8):
            pa, pb = rng.integers(0, W, 8192), rng.integers(0, W, 8192); pc = ((pa * pb >> 5) + pa + 37 * pb) & (W - 1); k = good[q, g]
            yes = np.flatnonzero(~k[pa] & ~k[pb] & k[pc] & (pa != pb)); no = np.flatnonzero((k[pa] | k[pb]) & (pa != pb))
            n = rng.choice(np.array([0, 1, CA - 1, CA, CA + 1, 16]), P); n[P - 1] = CA; n[0] = 16; n[2] = CA + 1
            m = np.argsort(rng.random((P, 16)), axis=1) < n[:, None]
            i = np.where(m, yes[rng.integers(0, len(yes), (P, 16))], no[rng.integers(0, len(no), (P, 16))]); aa, bb = pa[i], pb[i]
            kp = rng.integers(0, 12, P); kp[0] = 9; kp[P - 1] = 9; kp[2] = 9; kp[1] = 2; kp[P - 2] = 3; kp[3] = 0; kp[P - 3] = 1
            s = (kp == 0) | (kp == 2) | (kp == 3); aa[s] = own[s]; bb[s] = own[s]
            e = (W - 1) * rng.integers(0, 2, (P, 16)); aa[kp == 1] = e[kp == 1]; bb[kp == 1] = e[kp == 1]
            aa[kp == 4] = e[kp == 4]; bb[kp == 4] = W - 1 - e[kp == 4]
            slot = rng.integers(0, 16, P)
            for c, col in ((2, W - 3), (3, W - 2)):
                r = np.flatnonzero(kp == c); aa[r, slot[r]] = W - 4; bb[r, slot[r]] = col; z[q, g][:, r] = x[q, g, :, col][:, None]
            a[q, g] = aa.reshape(-1); b[q, g] = bb.reshape(-1)
    b[1] = a[1]
    w[:, 0] = 0; w[:, 1] = 15; w[:, 2] = 0; w[:, 2, 15] = 15; w[:, 3] = 15 * rng.integers(0, 2, (N, 16))
    return pack(x, z, w, a, b)
def setup_inputs_ends(rng):
    kind = rng.integers(0, 4, (N, 8, 1, W)); x = 255 * np.where(kind > 1, rng.integers(0, 2, (N, 8, 16, W)), kind)
    x = np.where((kind == 3) & (rng.random(x.shape) < 0.25), x ^ 1, x)
    hi = np.arange(8) & 1
    x[..., 0] = 255 * (1 - hi)[None, :, None]; x[..., W - 1] = 255 * hi[None, :, None]; x[0, ::2, :, W - 37] = 255
    cc = (((W - 1) * (W - 2) >> 5) + W - 1 + 37 * (W - 2)) & (W - 1)
    x[:, 1::2, :, W - 2] = 255; x[:, 1::2, :, cc] = 255
    zk = rng.integers(0, 3, (N, 8, 1, P)); z = 255 * np.where(zk == 2, rng.integers(0, 2, (N, 8, 16, P)), zk)
    w = 15 * rng.integers(0, 2, (N, 8, 16)); w[:, 1] = 15; w[:, 7] = 15; w[:, 2] = 0
    sh = (N, 8, NB)
    a = np.where(rng.random(sh) < 0.8, (W - 1) * rng.integers(0, 2, sh), rng.integers(0, W, sh))
    b = np.where(rng.random(sh) < 0.8, (W - 1) * rng.integers(0, 2, sh), rng.integers(0, W, sh))
    n = rng.integers(10, 17, (8, P, 1)); n[:, 0] = 16; n[:, P - 1] = 16
    m = (np.argsort(rng.random((8, P, 16)), axis=-1) < n).reshape(8, NB); top = ((W - 1) * hi)[:, None]
    a[0] = np.where(m, top, a[0]); b[0] = np.where(m, W - 1 - top, b[0])
    z[0] = 255 * (np.argsort(rng.random((8, 16, P)), axis=1) < rng.integers(0, 7, (8, 1, P)))
    for q in range(1, N):
        for g in (1, 7):
            for i, va, vb, vz in ((0, 0, W - 1, 255), (P - 1, 0, W - 1, 255), (1, W - 1, 0, 0), (P - 2, W - 1, 0, 0), (2, W - 1, W - 2, 0), (P - 3, W - 1, W - 2, 0)):
                a[q, g, 16 * i:16 * i + 16] = va; b[q, g, 16 * i:16 * i + 16] = vb; z[q, g, :, i] = vz
    return pack(x, z, w, a, b)
def setup_inputs_spread(rng):
    x, z, w, a, b = parts(rng)
    x = (np.exp2(8 * rng.random((N, 8, 1, W))) * rng.random(x.shape)).astype(np.int64)
    z = (np.exp2(8 * rng.random((N, 8, 1, P))) * rng.random(z.shape)).astype(np.int64)
    w = w >> rng.integers(0, 5, w.shape)
    a = (W * rng.random(a.shape) ** rng.integers(1, 5, (N, 8, 1))).astype(np.int64); b = (W * rng.random(b.shape) ** rng.integers(1, 5, (N, 8, 1))).astype(np.int64)
    return pack(x, z, w, np.minimum(a, W - 1), np.minimum(b, W - 1))
def setup_inputs_ties(rng):
    x, z, w, a, b = parts(rng)
    base = rng.integers(0, 256, (N, 8, 16, 6)); base[:, ::2] = rng.choice(np.array([0, 1, 128, 254, 255]), (N, 4, 16, 6))
    x = np.take_along_axis(base, rng.integers(0, 6, (N, 8, 1, W)), 3)
    z = np.where(rng.random((N, 8, 1, P)) < 0.75, np.take_along_axis(base, rng.integers(0, 6, (N, 8, 1, P)), 3), z)
    m = rng.random((N, 8, P, 1)) < 0.25
    a = a.reshape(N, 8, P, 16); b = b.reshape(N, 8, P, 16); b = np.where(rng.random(b.shape) < 0.125, a, b)
    a = np.where(m, a[..., :1], a).reshape(N, 8, NB); b = np.where(m, b[..., :1], b).reshape(N, 8, NB)
    return pack(x, z, w, a, b)
def check_inputs(d):
    bad = []
    for k, lo, hi in (("xt", 0, 255), ("zp", 0, 255), ("wl", 0, 15), ("ba", 0, W - 1), ("bb", 0, W - 1)):
        v = np.asarray(d[k]).astype(np.float64)
        if not np.all((v >= lo) & (v <= hi) & (v == np.floor(v))): bad.append("range of " + k)
    return bad
def reference(xt, zp, wl, ba, bb):
    X = xt.astype(np.float32).astype(np.int32).reshape(N, 8, 16, W); z = zp.astype(np.float32).astype(np.int32).reshape(N, 8, 16, P)
    w = wl.astype(np.float32).astype(np.int32).reshape(N, 8, 16, 1)
    L = [np.stack([gentries(v) for v in m]).astype(np.int32) for m in (ba, bb)]
    I = np.zeros((N, 8, NB), np.int32); G = np.zeros((N, 8, NB), np.int32); rej = [0] * N
    def before(m):
        m = m.astype(np.int32).reshape(8, P, 16)
        return (np.add.accumulate(m, axis=2) - m).reshape(8, NB)
    for t in range(T):
        now = [0] * N
        for q in range(N):
            s = (q + t) % N
            H = L[t % 2][q]; O = L[1 - t % 2][q]; C = ((H * O >> 5) + H + 37 * O) & (W - 1)
            h, o, c = [np.take_along_axis(X[s], v[:, None, :], 2) for v in (H, O, C)]
            zz = np.repeat(z[q], 16, axis=2); dh, do, dc = [np.add.reduce(np.abs(v - zz), axis=1) for v in (h, o, c)]
            live = H != O
            rec = live & (do <= np.minimum(dh, dc))
            want = live & ~rec & (dc < dh) & (G[q] < LG); am = want & (before(want) < CA)
            ins = live & ~rec & ~am
            ch = np.where(rec[:, None, :], o, np.where(am[:, None, :], c, h))
            V = np.add.reduce((ch - h).reshape(8, 16, P, 16), axis=3)
            ok = np.add.reduce((V >= 0).astype(np.int32), axis=1) >= LV
            now[s] = int(np.add.reduce((~ok).astype(np.int64), axis=None)); yes = np.repeat(ok, 16, axis=1)
            I[q] += ins | ((rec | am) & ~yes); G[q] += am & yes
            H2 = np.where(yes & rec, O, np.where(yes & am, C, H))
            sp = I[q] >= LI; v = np.where((before(sp) & 1) == 1, C, H)
            H2 = np.where(sp, v, H2); O2 = np.where(sp, v, O); I[q] = np.where(sp, 0, I[q])
            M = np.maximum.reduce(ch.reshape(8, 16, P, 16), axis=3); u = np.add.reduce(w[s] * M, axis=1) & (W - 1)
            O2 = np.where(live, O2, ((H * np.repeat(u, 16, axis=1) >> 5) + H + rej[s]) & (W - 1))
            L[t % 2][q] = H2; L[1 - t % 2][q] = O2
            if t < T - 1:
                z[q] = np.abs(z[q] - M)
                at = (S * np.arange(P)[None, :] + (u & (S - 1)))[:, None, :]
                np.put_along_axis(X[s], at, (np.take_along_axis(X[s], at, 2) + M) >> 1, 2)
        rej = now
    home = [(s - (T - 1)) % N for s in range(N)]
    ya, yb, yi, yg = [np.stack([gtable(m[q]) for q in home]).astype(np.float32) for m in (L[0], L[1], I, G)]
    return {"ya": ya, "yb": yb, "yi": yi, "yg": yg}

@@ -1,0 +1,559 @@
+from concourse.bass import DstId, RemoteDMATransfer
+from concourse.mybir import AluOpType, AxisListType, ActivationFunctionType
+
+OP = AluOpType
+AF = ActivationFunctionType
+W, NP, NREAD = 4096, 256, 6
+BLOCKS = [128, 128]
+SLOT = 128
+CY = 0.00083
+PECY = 0.00042
+PEO = 0.02
+VO = 0.05
+GR = 1.6
+WIN = 0.15
+PIECES = 2
+MODE = [{"h": "AA", "o": "FF", "c": "FF"}, {"h": "AA", "o": "FF", "c": "FF"}]
+CHQ = ["AV", "AV"]
+SPLIT = "c"
+VH = 8
+SEED = 1
+NOISE = 0.0
+LEADS = (0.0, 2.0, 3.0, 4.5, 6.0)
+PASSES = 25
+WAKE = 0.1
+NETT = 5.0
+
+DTY = {"aw": ("bfloat16", 2), "af": ("float32", 4), "ai": ("int32", 4), "au": ("uint16", 2), "ah": ("float16", 2)}
+_size = {k: 0 for k in DTY}
+
+
+def new(ar, n):
+    a = _size[ar]
+    step = 32 // DTY[ar][1]
+    _size[ar] = a + (n + step - 1) // step * step
+    return (ar, a, a + n, 1)
+
+
+def sub(h, a, b, s=1):
+    return (h[0], h[1] + a, h[1] + b, s)
+
+
+def ps(bank, slot, n):
+    return ("ps%d" % bank, slot * SLOT, slot * SLOT + n, 1)
+
+
+def ncol(h):
+    return (h[2] - h[1] + h[3] - 1) // h[3]
+
+
+def wide(h):
+    return 4 if h[0] not in DTY else DTY[h[0]][1]
+
+
+def build():
+    ops = []
+    NB = len(BLOCKS)
+    cur = [-1, 0]
+
+    def add(eng, cost, reads, writes, emit, name="", kind="c", sem=None, extra=()):
+        ops.append({"e": eng, "c": cost, "r": reads, "w": writes, "f": emit, "n": name, "k": kind, "s": sem, "x": list(extra), "t": cur[0], "blk": cur[1]})
+        return len(ops) - 1
+
+    def vts(o, i, s1, s2, op0, op1=None, name="ts"):
+        n = ncol(o)
+        fast = wide(o) == 2 and wide(i) == 2
+        rd = [i] + [s for s in (s1, s2) if isinstance(s, tuple)]
+
+        def f(q, V):
+            a = V(s1) if isinstance(s1, tuple) else s1
+            if op1 is None:
+                return q.tensor_scalar(V(o), V(i), a, None, op0)
+            b = V(s2) if isinstance(s2, tuple) else s2
+            return q.tensor_scalar(V(o), V(i), a, b, op0, op1)
+        return add("V", 0.03 + CY * max(64, n * (0.5 if fast else 1)), rd, [o], f, name)
+
+    def vtt(o, a, b, op, name="tt"):
+        n = ncol(o)
+        both = a[0] in DTY and b[0] in DTY
+        return add("V", 0.03 + CY * max(64, n * (2 if both else 1)), [a, b], [o], lambda q, V: q.tensor_tensor(V(o), V(a), V(b), op), name)
+
+    def vcopy(o, i, name="cp"):
+        n = ncol(o)
+        fast = wide(o) == 2 and wide(i) == 2
+        return add("V", 0.03 + CY * max(64, n * (0.5 if fast else 1)), [i], [o], lambda q, V: q.tensor_copy(V(o), V(i)), name)
+
+    def vset(o, v):
+        return add("V", 0.03 + CY * max(64, ncol(o) * (0.5 if wide(o) == 2 else 1)), [], [o], lambda q, V: q.memset(V(o), v), "set")
+
+    def act(o, i, fn, scale=1.0, bias=0.0, acc=None, name="act"):
+        def f(q, V):
+            if acc is None:
+                return q.activation(V(o), V(i), fn, bias, scale)
+            return q.activation(V(o), V(i), fn, bias, scale, accum_out=V(acc))
+        return add("A", 0.06 + CY * ncol(o), [i], [o] + ([acc] if acc else []), f, name)
+
+    def gath(eng, o, win, off, minus=None, op=None, name="gather"):
+        n = ncol(o)
+        if eng == "A":
+            return add("A", 0.07 + CY * GR * n, [win, off], [o],
+                       lambda q, V: q.activation(V(o), V(win).indirect(V(off)), AF.Copy), name)
+        if minus is None:
+            return add("V", 0.05 + CY * GR * n, [win, off], [o],
+                       lambda q, V: q.tensor_copy(V(o), V(win).indirect(V(off))), name)
+        return add("V", 0.05 + CY * GR * n, [win, off, minus], [o],
+                   lambda q, V: q.tensor_tensor(V(o), V(win).indirect(V(off)), V(minus), op), name)
+
+    def pe(o, terms, name="pe", first=True, stop=True, extra=()):
+        c = 0.03
+        for l, r in terms:
+            c += PEO + PECY * max(64, ncol(r)) * (4 if l[0] == "af" else 1)
+
+        def f(q, V):
+            last = None
+            for k, (l, r) in enumerate(terms):
+                last = q.matmul(V(o), V(l), V(r), first and k == 0, stop and k == len(terms) - 1)
+            return last
+        return add("P", c, [x for t in terms for x in t], [o], f, name, extra=[i for i in extra if i is not None])
+
+    def mailto(src, land, nm, t, b):
+        sem = "%s%d_%d" % (nm, t, b)
+        k = add("G", 1.0, [src], [], ("send", src, land, sem), nm, "send")
+        add("N", NETT, [], [land], None, nm, "net", sem, (k,))
+
+    X = new("aw", W)
+    xin, zin, win_ = X, new("aw", NP), new("aw", 1)
+    bain, bbin = new("ai", NP), new("ai", NP)
+    for k, (nm, h, q) in enumerate((("ba", bain, "S"), ("bb", bbin, "S"), ("zp", zin, "S"), ("wl", win_, "S"), ("xt", X, "S"))):
+        add(q, 0.1, [], [h], lambda q, V, nm=nm, h=h: q.dma_start(V(h), V(nm)), "ld" + nm, "dma", "ld" + nm)
+
+    ONE = new("aw", 128)
+    ID, NEG, BO, LT, L64, L4, T1 = [new("aw", 128) for _ in range(7)]
+    MID = {v: new("aw", 128) for v in (-64, -2, 4, 2048, -4096, 528384, -2 ** 23, 2 ** 30, 65536, 98304)}
+    D, WD = new("aw", 144), new("aw", 144)
+    WB, WB64 = new("aw", 128), new("aw", 128)
+    HI, H65, H101, H32, HH = [new("ah", 128) for _ in range(5)]
+    MONE = new("aw", max(BLOCKS))
+    IF = new("af", 128)
+    NCM = max(BLOCKS) // 16
+    MASK = new("aw", 16 * max(BLOCKS))
+
+    def asel(o, i, pat, cmp, base, cm):
+        return add("G", 0.4, [i], [o], lambda q, V: q.affine_select(V(o), V(i), pat, cmp, 0.0, base, cm), "asel")
+    vset(ONE, 1.0)
+    asel(ID, ONE, [[-1, 128]], OP.is_equal, 0, 1)
+    asel(T1, ONE, [[-16, 8], [0, 16]], OP.is_ge, 0, 1)
+    asel(BO, T1, [[16, 8], [0, 16]], OP.is_ge, 15, -1)
+    asel(LT, BO, [[1, 128]], OP.is_gt, 0, -1)
+    B1, B2, BASE = new("ai", NCM), new("ai", NCM), new("ai", NCM)
+    add("G", 0.2, [], [B1], lambda q, V: q.iota(V(B1), [[0, NCM]], 0, 16), "iota")
+    add("G", 0.2, [], [B2], lambda q, V: q.iota(V(B2), [[256, NCM]], 0, 0), "iota")
+    vts(B1, B1, 255, None, OP.bitwise_and)
+    vtt(BASE, B1, B2, OP.add)
+    vcopy(HI, ID)
+    vts(H65, ID, 2080.0, None, OP.mult)
+    vts(H101, ID, 3232.0, None, OP.mult)
+    vts(H32, ID, 32.0, None, OP.mult)
+    vts(NEG, ID, -1.0, None, OP.mult)
+    for v in sorted(MID):
+        act(MID[v], ID, AF.Copy, scale=float(v))
+    act(IF, ID, AF.Copy)
+    vtt(L64, LT, MID[-64], OP.add)
+    vtt(L4, LT, MID[4], OP.add)
+    vset(D, 0.0)
+    vcopy(sub(D, 15, 143, 16), sub(BO, 0, 128, 16))
+    WF = new("af", 1)
+    vcopy(WF, win_)
+    vts(WD, D, WF, None, OP.mult)
+    vts(WB, BO, WF, None, OP.mult)
+    vts(WB64, WB, 2048.0, None, OP.mult)
+    vset(MONE, -1.0)
+    vts(HH, ID, 0.5, None, OP.mult)
+    vset(MASK, 1.0)
+    vset(sub(MASK, 0, 16 * max(BLOCKS), 16), 0.0)
+
+    p0 = [sum(BLOCKS[:b]) for b in range(NB)]
+    big = []
+    for b in range(NB):
+        n = BLOCKS[b]
+        d = {k: new("aw", 16 * n) for k in ("h", "o", "c", "ch", "ah", "zx", "zs")}
+        d.update({k: new("aw", n) for k in ("live", "rec", "want", "am", "sv", "jk", "ry", "ay", "spl", "fl", "so", "fu")})
+        d.update({k: new("ah", n) for k in ("Hc", "Oc", "Cc", "tO", "tC", "tH", "s1", "s2")})
+        d.update({k: new("af", n) for k in ("dhS", "m", "gl", "dhG", "m2", "stU", "xg", "P", "pU")})
+        d.update({k: new("ai", n) for k in ("T", "C", "TU", "xf")})
+        d.update({k: new("ai", n // 16) for k in ("ui", "ua", "ul")})
+        d["C16"], d["ch16"], d["l16"] = new("au", n), new("au", n), new("au", n // 16)
+        vset(d["zs"], 0.0)
+        big.append(d)
+    ACC = new("af", 16 * NREAD)
+    RM = [[new("aw", 128) for _ in range(NB)] for _ in range(2)] * 3
+    subn = [0]
+    lastv = [None]
+
+    mail = []
+    for b in range(NB):
+        n = BLOCKS[b]
+        A16, B16, I0, G0 = new("au", n), new("au", n), new("aw", n), new("aw", n)
+        vcopy(A16, sub(bain, p0[b], p0[b] + n))
+        vcopy(B16, sub(bbin, p0[b], p0[b] + n))
+        vset(I0, 0.0)
+        vset(G0, 0.0)
+        mail.append((A16, B16, sub(zin, p0[b], p0[b] + n), I0, G0))
+
+    for t in range(NREAD):
+        last = t == NREAD - 1
+        nxt = []
+        for b in range(NB):
+            cur[0], cur[1] = t, b
+            n, d, par = BLOCKS[b], big[b], b & 1
+            H16, O16, z, I, G = mail[b][t & 1], mail[b][1 - (t & 1)], mail[b][2], mail[b][3], mail[b][4]
+            hp, lin = ps(2, 2 * par, n), ps(2, 2 * par + 1, n)
+            sg = ps(3 + par, 3, n)
+            vts(d["Hc"], H16, -2048.0, None, OP.add, name="Hc")
+            vts(d["Oc"], O16, -2048.0, None, OP.add, name="Oc")
+            pe(hp, [(HI, d["Hc"])], "HcPS")
+            pe(lin, [(H65, d["Hc"]), (H101, d["Oc"])], "lin")
+            vtt(d["P"], d["Oc"], hp, OP.mult, "P")
+            vtt(d["T"], d["P"], lin, OP.add, "T")
+            vts(d["C"], d["T"], 5, 4095, OP.arith_shift_right, OP.bitwise_and, name="C")
+            vcopy(d["C16"], d["C"], "C16")
+            vts(d["Cc"], d["C16"], -2048.0, None, OP.add, name="Cc")
+            vtt(d["live"], d["Oc"], hp, OP.not_equal, "live")
+            act(sub(d["zs"], 0, 16 * n, 16), z, AF.Copy, name="zs")
+            mk = sub(MASK, 0, 16 * n)
+            add("V", 0.03 + CY * 8 * n, [mk, d["zs"]], [d["zx"]],
+                lambda q, V, mk=mk, d=d: q.tensor_tensor_scan(V(d["zx"]), V(mk), V(d["zs"]), 0.0, OP.mult, OP.add), "zx")
+            act(sg, G, AF.Sign, scale=-1.0, bias=1.5, name="sg")
+            vtt(d["gl"], d["live"], sg, OP.mult, "gl")
+        for b in range(NB):
+            cur[0], cur[1] = t, b
+            n, d, par = BLOCKS[b], big[b], b & 1
+            H16, O16, z, I, G = mail[b][t & 1], mail[b][1 - (t & 1)], mail[b][2], mail[b][3], mail[b][4]
+            dh, do, dc, cap = [ps(3 + par, k, n) for k in range(4)]
+            vs = ps(5, b, n)
+            pc = [(k * n // PIECES, (k + 1) * n // PIECES) for k in range(PIECES)]
+            for k, lst, dist in (("h", H16, dh), ("o", O16, do), ("c", d["C16"], dc)):
+                res = d["ah"] if k == "h" else d[k]
+                for (q0, q1), mode in zip(pc, MODE[b][k]):
+                    e0, e1 = 16 * q0, 16 * q1
+                    if mode == "F":
+                        gath("V", sub(d[k], e0, e1), X, sub(lst, q0, q1), sub(d["zx"], e0, e1), OP.subtract, k)
+                        act(sub(res, e0, e1), sub(d[k], e0, e1), AF.Abs, name="abs" + k)
+                        continue
+                    gath(mode, sub(d[k], e0, e1), X, sub(lst, q0, q1), name=k)
+                    for a0 in range(e0, e1, 512):
+                        a1 = min(a0 + 512, e1)
+                        tile = ("ps%d" % (subn[0] & 1), 0, a1 - a0, 1)
+                        subn[0] += 1
+                        pe(tile, [(ID, sub(d[k], a0, a1)), (NEG, sub(d["zx"], a0, a1))], "sub")
+                        act(sub(res, a0, a1), tile, AF.Abs, name="abs" + k)
+                for q0, q1 in (pc if k in SPLIT else [(0, n)]):
+                    pe(sub(dist, q0, q1), [(sub(D, 15 - j, 143 - j), sub(res, 16 * q0 + j, 16 * q1, 16)) for j in range(16)], "d" + k)
+                if k == "h":
+                    for j0 in range(0, 16, VH):
+                        terms = [(NEG, sub(d["h"], j, 16 * n, 16)) for j in range(j0, j0 + VH)]
+                        pe(vs, terms, "voteh", first=j0 == 0, stop=False, extra=lastv)
+            act(d["dhS"], dh, AF.Copy, name="dhS")
+            vtt(d["dhG"], d["gl"], dh, OP.mult, "dhG")
+            vtt(d["m2"], d["dhG"], do, OP.min, "m2")
+            vtt(d["m"], d["dhS"], dc, OP.min, "m")
+            vtt(d["want"], d["m2"], dc, OP.is_gt, "want")
+            vtt(d["rec"], d["m"], do, OP.is_ge, "rec")
+            pe(cap, [(L64, d["want"])], "cap")
+            vts(d["am"], cap, -60.0, None, OP.is_lt, name="am")
+            rp, ap_, sp_, cs = dh, do, dc, cap
+            pe(rp, [(ID, d["rec"])], "recPS")
+            vtt(d["tO"], d["Oc"], rp, OP.mult, "tO")
+            pe(ap_, [(ID, d["am"])], "amPS")
+            pe(sp_, [(ID, sub(ONE, 0, n)), (NEG, d["rec"]), (NEG, d["am"])], "sH")
+            vtt(d["tC"], d["Cc"], ap_, OP.mult, "tC")
+            vtt(d["tH"], d["Hc"], sp_, OP.mult, "tH")
+            pe(cs, [(HI, d["tO"]), (HI, d["tC"]), (HI, d["tH"])], "chS")
+            vts(d["ch16"], cs, 2048.0, None, OP.add, name="ch16")
+            for (q0, q1), e in zip(pc, CHQ[b]):
+                gath(e, sub(d["ch"], 16 * q0, 16 * q1), X, sub(d["ch16"], q0, q1), name="ch")
+            lastv[0] = pe(vs, [(ID, sub(d["ch"], j, 16 * n, 16)) for j in range(16)], "vote", first=False)
+        for b in range(NB):
+            cur[0], cur[1] = t, b
+            n, d, par = BLOCKS[b], big[b], b & 1
+            z = mail[b][2]
+            mx = d["zx"]
+            for k in range(PIECES):
+                q0, q1 = 16 * (k * n // PIECES), 16 * ((k + 1) * n // PIECES)
+                mk, cp, mp = sub(MASK, 0, q1 - q0), sub(d["ch"], q0, q1), sub(mx, q0, q1)
+                add("V", VO + CY * (q1 - q0) / 2, [mk, cp], [mp],
+                    lambda q, V, mk=mk, cp=cp, mp=mp: q.tensor_tensor_scan(V(mp), V(mk), V(cp), 0.0, OP.mult, OP.max), "mx")
+            M = sub(mx, 15, 16 * n, 16)
+            ur, uc = ps(6, 2 * par, n), ps(6, 2 * par + 1, n)
+            d["M"], d["ur"], d["uc"] = M, ur, uc
+            out = {}
+            if not last:
+                out["AB"] = new("au", 2 * n)
+                out["ZIG"] = new("aw", 3 * n)
+                out["A"], out["B"] = sub(out["AB"], 0, n), sub(out["AB"], n, 2 * n)
+                out["z"], out["I"], out["G"] = [sub(out["ZIG"], k * n, (k + 1) * n) for k in range(3)]
+                ulp = sub(uc, 0, n // 16)
+                pe(ulp, [(sub(WD, 15 - j, 143 - j), sub(mx, 15 + 16 * j, 16 * n, 256)) for j in range(16)], "ulist")
+                vcopy(d["ui"], ulp, "ui")
+                vts(d["ua"], d["ui"], 15, None, OP.bitwise_and, name="ua")
+                vtt(d["ul"], d["ua"], sub(BASE, 0, n // 16), OP.add, "ul")
+                vcopy(d["l16"], d["ul"], "l16")
+                xw = sub(X, 16 * p0[b], 16 * (p0[b] + n))
+                gath("V", d["xg"], xw, d["l16"], M, OP.add, "xg")
+                vts(d["xf"], d["xg"], -0.5, 0.5, OP.add, OP.mult, name="xf")
+                add("V", 0.05 + CY * 3.8 * n, [d["xf"], d["l16"]], [xw],
+                    lambda q, V, d=d, xw=xw: q.tensor_copy(V(xw).indirect(V(d["l16"])), V(d["xf"])), "scat")
+            else:
+                out["A"], out["B"], out["I"], out["G"] = [new("af", n) for _ in range(4)]
+            d["out"] = out
+        for b in range(NB):
+            cur[0], cur[1] = t, b
+            n, d, par = BLOCKS[b], big[b], b & 1
+            H16, O16, z, I, G = mail[b][t & 1], mail[b][1 - (t & 1)], mail[b][2], mail[b][3], mail[b][4]
+            out, M, ur, uc = d["out"], d["M"], d["ur"], d["uc"]
+            one = sub(ONE, 0, n)
+            S0, S1, S2, S3 = [ps(3 + par, k, n) for k in range(4)]
+            vs, cn = ps(5, b, n), S3
+            old0, old1 = ps(2, 2 * par, n), ps(2, 2 * par + 1, n)
+            yes, nm = ps(7, 2 * par, n), ps(7, 2 * par + 1, n)
+            act(d["sv"], vs, AF.Sign, bias=0.5, name="sv")
+            pe(cn, [(BO, d["sv"])], "cnt")
+            acc = sub(ACC, 16 * t + b, 16 * t + b + 1)
+            act(yes, cn, AF.Sign, bias=0.5, acc=None if last else acc, name="yes")
+            if not last:
+                rm = RM[t][b]
+                add("A", 0.06 + CY * 128, [ONE, acc], [rm], lambda q, V, rm=rm, acc=acc: q.activation(V(rm), V(ONE), AF.Copy, 0.0, V(acc)), "RM")
+                pe(old1, [(ID, z), (NEG, M)], "zd")
+                act(out["z"], old1, AF.Abs, name="z")
+            vtt(d["ry"], d["rec"], yes, OP.is_equal, "ry")
+            vtt(d["ay"], d["am"], yes, OP.is_equal, "ay")
+            pe(old0, [(ID, G), (ID, d["ay"])], "Gs")
+            act(out["G"], old0, AF.Copy, name="G")
+            pe(S0, [(ID, d["ry"]), (ID, d["ay"])], "mv")
+            vtt(nm, d["live"], S0, OP.is_gt, "nm")
+            vtt(out["I"], I, nm, OP.not_equal, "I")
+            vtt(d["spl"], I, nm, OP.mult, "spl")
+            if not last:
+                zl, lh, lo = new("aw", 3 * n), new("au", n), new("au", n)
+                mailto(out["ZIG"], zl, "rz", t, b)
+            pe(S1, [(LT, d["spl"])], "bef")
+            act(d["fl"], S1, AF.Copy, scale=0.5, bias=128.75, name="fl")
+            pe(S2, [(L4, d["spl"]), (MID[-2], d["fl"])], "par")
+            vts(d["so"], S2, -253.5, None, OP.is_gt, name="so")
+            pe(S3, [(ID, one), (NEG, d["ry"]), (NEG, d["ay"]), (NEG, d["so"])], "sH2")
+            pe(S0, [(ID, d["ay"]), (ID, d["so"])], "a2")
+            vtt(d["s1"], d["tO"], yes, OP.mult, "tO2")
+            vtt(d["tC"], d["Cc"], S0, OP.mult, "tC2")
+            vtt(d["tH"], d["Hc"], S3, OP.mult, "tH2")
+            pe(S1, [(HH, d["tO"]), (HH, d["s1"]), (HI, d["tC"]), (HI, d["tH"])], "nHs")
+            oh, oo = (out["A"], out["B"]) if t % 2 == 0 else (out["B"], out["A"])
+            vts(oh, S1, 2048.0, None, OP.add, name="nH")
+            if not last:
+                mailto(oh, lh, "rh", t, b)
+            pe(ur, [(WB, M)], "uraw")
+            act(d["fu"], ur, AF.Copy, scale=1.0 / 4096, bias=128.5 + 1.0 / 8192, name="fu")
+            pe(uc, [(MID[528384], one), (MID[-4096], d["fu"]), (WB, M)], "u")
+            lin = [(WB64, M), (MID[-2 ** 23], d["fu"]), (MID[2 ** 30], one), (H32, d["Hc"]), (MID[98304 if t else 65536], one)]
+            if t > 0:
+                lin += [(RM[t - 1][k], sub(MONE, 0, n)) for k in range(NB)]
+            vtt(d["pU"], d["Hc"], uc, OP.mult, "pU")
+            pe(ur, lin, "linU")
+            vtt(d["TU"], d["pU"], ur, OP.add, "TU")
+            vts(d["TU"], d["TU"], 5, 4095, OP.arith_shift_right, OP.bitwise_and, name="U")
+            pe(S3, [(ID, d["live"]), (NEG, d["spl"])], "sO")
+            pe(S0, [(ID, one), (NEG, d["live"])], "st")
+            vtt(d["stU"], d["TU"], S0, OP.mult, "stU")
+            vtt(d["s2"], d["Oc"], S3, OP.mult, "s2")
+            vtt(d["s1"], d["spl"], S1, OP.mult, "s1")
+            pe(S2, [(MID[2048], d["live"]), (IF, d["stU"]), (HI, d["s2"]), (HI, d["s1"])], "nOs")
+            vcopy(oo, S2, "nO")
+            if not last:
+                mailto(oo, lo, "ro", t, b)
+                nxt.append(((lh, lo) if t % 2 == 0 else (lo, lh)) + (sub(zl, 0, n), sub(zl, n, 2 * n), sub(zl, 2 * n, 3 * n)))
+            else:
+                for k, nme in (("G", "yg"), ("I", "yi"), ("A", "ya"), ("B", "yb")):
+                    add("S", 0.1, [out[k]], [], lambda q, V, nme=nme, h=out[k], a=p0[b], n=n: q.dma_start(V(nme)[:, a:a + n], V(h)), "st" + nme, "dma", "st%s%d" % (nme, b))
+        mail = nxt
+    return ops
+
+
+def depend(ops):
+    hist = {}
+    for i, o in enumerate(ops):
+        dep = set(o["x"])
+        for h, w in [(h, 0) for h in o["r"]] + [(h, 1) for h in o["w"]]:
+            for j, a, b, jw in hist.get(h[0], ()):
+                if (w or jw) and a < h[2] and h[1] < b:
+                    dep.add(j)
+        for h, w in [(h, 0) for h in o["r"]] + [(h, 1) for h in o["w"]]:
+            lst = hist.setdefault(h[0], [])
+            if w:
+                lst[:] = [e for e in lst if not (h[1] <= e[1] and e[2] <= h[2] and h[3] == 1)]
+            lst.append((i, h[1], h[2], w))
+        dep.discard(i)
+        o["d"] = sorted(dep)
+        o["b"] = sorted({h[0] for h in o["r"] + o["w"] if h[0] not in DTY})
+
+
+LDT = {"ldba": 3.0, "ldbb": 3.2, "ldzp": 3.4, "ldwl": 3.4, "ldxt": 7.0}
+
+
+def schedule(ops, pri, pred, succ):
+    n = len(ops)
+    left = [len(p) for p in pred]
+    ready = {}
+    est = [0.0] * n
+    free, bank = {}, {}
+    end, start = [0.0] * n, [0.0] * n
+    for i in range(n):
+        if not left[i]:
+            ready.setdefault(ops[i]["e"], []).append(i)
+    order, done = [], 0
+    while done < n:
+        best = None
+        for e, lst in ready.items():
+            if not lst:
+                continue
+            t0 = free.get(e, 0.0) if e != "N" else 0.0
+            cand = []
+            for i in lst:
+                s = max(t0, est[i])
+                for b in ops[i]["b"]:
+                    for e2, u in bank.get(b, {}).items():
+                        if e2 != e:
+                            s = max(s, u + WAKE)
+                cand.append((s, -pri[i], i))
+            s0 = min(cand)[0]
+            c = min((c for c in cand if c[0] <= s0 + WIN), key=lambda c: c[1])
+            if best is None or c[0] < best[0]:
+                best = (c[0], c[2], e)
+        s, i, e = best
+        ready[e].remove(i)
+        o = ops[i]
+        start[i] = s
+        end[i] = s + o["c"]
+        fin = end[i]
+        if o["k"] == "dma":
+            fin = s + LDT.get(o["n"], 2.5)
+        free[e] = end[i]
+        for b in o["b"]:
+            bank.setdefault(b, {})[e] = end[i]
+        order.append(i)
+        done += 1
+        for j in succ[i]:
+            est[j] = max(est[j], fin + (WAKE if ops[j]["e"] != e else 0.06))
+            left[j] -= 1
+            if not left[j]:
+                ready.setdefault(ops[j]["e"], []).append(j)
+        end[i] = fin
+    return order, start, end
+
+
+def plan(ops):
+    n = len(ops)
+    pred = [o["d"] for o in ops]
+    succ = [[] for _ in ops]
+    for i in range(n):
+        for j in pred[i]:
+            succ[j].append(i)
+    path = [0.0] * n
+    for i in range(n - 1, -1, -1):
+        path[i] = ops[i]["c"] + max([path[j] + WAKE for j in succ[i]], default=0.0)
+    best = None
+    seed = [SEED]
+
+    def rnd():
+        seed[0] = (seed[0] * 1103515245 + 12345) % 2147483648
+        return seed[0] / 1073741824.0 - 1.0
+
+    for lead in LEADS:
+        pri = [p + (lead if o["t"] >= 0 and o["blk"] == 0 else 0.0) for p, o in zip(path, ops)]
+        for _ in range(PASSES):
+            order, start, end = schedule(ops, pri, pred, succ)
+            if best is None or max(end) < max(best[2]):
+                best = (order, start, end)
+            back = schedule(ops, end, succ, pred)[2]
+            pri = [x + NOISE * rnd() for x in back]
+    return best
+
+
+OPS = build()
+depend(OPS)
+ORDER, START, END = plan(OPS)
+
+SCRATCH = {k: ("sbuf", [128, _size[k]], DTY[k][0]) for k in DTY}
+SCRATCH.update({"ps%d" % k: ("psum", [128, 512], "float32") for k in range(8)})
+SEMAPHORES = ["cV", "cA", "cP", "cG", "sent"] + sorted({o["s"] for o in OPS if o["s"]})
+
+
+def rank_program(g, core, T, topo):
+    rank = T.rank_of(core)
+    if rank is None:
+        return
+    dst = T.cores[(rank + 1) % len(T.cores)]
+    rid, pid, _ = topo.addr(dst)
+    mask = topo.mask(core, dst)
+    width = len(topo.engines(core, dst))
+    queue = {"V": g.vector, "A": g.scalar, "P": g.tensor, "G": g, "S": g.sync}
+
+    def V(h):
+        if isinstance(h, str):
+            return T[h][:]
+        if h[3] == 1:
+            return T[h[0]][:, h[1]:h[2]]
+        return T[h[0]][:, h[1]:h[2]:h[3]]
+
+    count = {e: 0 for e in "VAPG"}
+    know = {e: {} for e in queue}
+    snap = {}
+    lastb = {}
+    sent = 0
+    sig = {}
+
+    def need(e, i):
+        s, c = sig[i]
+        if know[e].get(s, 0) >= c:
+            return
+        queue[e].wait_ge(T.sem[s], c)
+        for k, v in snap[i].items():
+            if know[e].get(k, 0) < v:
+                know[e][k] = v
+        know[e][s] = c
+
+    for i in ORDER:
+        o = OPS[i]
+        e = o["e"]
+        if o["k"] == "net":
+            sig[i] = (o["s"], width)
+            snap[i] = {}
+            continue
+        deps = {j for j in o["d"] if OPS[j]["k"] != "send"}
+        for b in o["b"]:
+            for e2, j in lastb.get(b, {}).items():
+                if e2 != e:
+                    deps.add(j)
+        for j in sorted(deps, key=lambda j: -START[j]):
+            need(e, j)
+        if o["k"] == "send":
+            _s, src, land, sem = o["f"]
+            g.remote_dma(V(land), V(src), T.sem[sem], T.sem.sent, pid, rid, mask)
+            sent += width
+            continue
+        ins = o["f"](queue[e], V)
+        if o["k"] == "dma":
+            ins.then_inc(T.sem[o["s"]], 16)
+            sig[i] = (o["s"], 16)
+            snap[i] = dict(know[e])
+        else:
+            count[e] += 1
+            ins.then_inc(T.sem["c" + e], 1)
+            sig[i] = ("c" + e, count[e])
+            snap[i] = dict(know[e])
+            for b in o["b"]:
+                lastb.setdefault(b, {})[e] = i
+    for e in "VAPG":
+        g.wait_ge(T.sem["c" + e], count[e])
+    for i in ORDER:
+        if OPS[i]["k"] in ("dma", "net"):
+            g.wait_ge(T.sem[OPS[i]["s"]], sig[i][1])
+    g.wait_ge(T.sem.sent, sent)

@@ -1,46 +1,55 @@
+import math
 from concourse.bass import DstId, RemoteDMATransfer
 from concourse.mybir import AluOpType, AxisListType, ActivationFunctionType
 
 OP = AluOpType
 AF = ActivationFunctionType
 W, NP, NREAD = 4096, 256, 6
-BLOCKS = [128, 128]
+NB, n = 2, 128
+SEG = 17 * n
 SLOT = 128
+BIG = 8192.0
 CY = 0.00083
 PECY = 0.00042
-PEO = 0.02
-VO = 0.05
-GR = 1.6
-WIN = 0.15
-PIECES = 2
-MODE = [{"h": "AA", "o": "FF", "c": "FF"}, {"h": "AA", "o": "FF", "c": "FF"}]
-CHQ = ["AV", "AV"]
-SPLIT = "c"
-VH = 8
-SEED = 1
-NOISE = 0.0
-LEADS = (0.0, 2.0, 3.0, 4.5, 6.0)
-PASSES = 25
-WAKE = 0.1
-NETT = 5.0
+PEO = 0.008
+VO, AO = 0.045, 0.06
+GR = 1.56
+NETT = 4.5
+SAME = 0.06
+TURN = """
+Hc0 h0 once1+ twice1+ Rt1+ Oc0 p11+ HcPS0 lin0 p21+ G1+ y1+ I1+ B21+ P0 rz1+ H11+ T0 pU1+ TU1+ h0b C0 H21+ U1+ C160 nO1+ c0 nH1+ h0c ro1+
+zx0 rawh0 c0b sideh0 st0 voteh0 fixh0 maxh0 o0b rawc0 sidec0 fixc0 dh0 Cc0 maxc0 zs1 o0 zx1 dc0 kt1+ voteh0b Hc1 K1+ Oc1 dhS0 sideo0 lin1
+h1b fixo0 rawo0 x0 maxo0 pen0 HcPS1 P1 do0 h1 T1 m0 mw0 zPS1 want0 At0 cntw0 C1 cap0 C161 DC0 am0 DO0 sideh1 c1 rec0 voteh1 fixh1 sel0
+sel20 rawh1 ch160 maxh1 ch0 voteh1b ch0b dh1 splt0 c1b Cc1 vote0 stK0 st1 mx0 vote0b stK1 mx0b g20 sv0 sidec1 o1 Mh0 fixc1 splt0b uraw0
+spl0 ulist0 maxc1 par0 rawc1 ui0 ua0 A0 dc1 fl0 sideo1 fu0 so0 dhS1 p20 o1b ryt0 x1 ayt0 fixo1 zd0 maxo1 u0 pen1 low0 B20 sideo1b ar0 ul0
+fixo1b rawo1 m1 z0 maxo1b l160 once0 twice0 Rt0 mw1 do1 xg0 p10 G0 y0 I0 pU0 rz0 H10 want1 TU0 cntw1 rec1 cap1 U0 H20 am1 nO0 sel1 nH0
+sel21 At1 ro0 ch161 DO1 ch1 ch1b ct0 splt1 DC1 g21 ch1c mx1b vote1 xf0 mx1 vote1b mx1c scat0 ulist1 sv1 yes0 splt1b ui1 ryt1 ua1 ct1
+uraw1 ul1 yes1 ayt1 fu1 l161 zPS0- spl1 xg1 Mh1 A1 par1 zs0- u1 xf1 fl1 scat1 ar1 zd1 z1 so1 low1
+"""
+CFG = {
+    "col": [{"h": "A4A2V2", "o": "A4A4", "c": "A4A4"}, {"h": "A4A4", "o": "A5A3", "c": "A4A4"}],
+    "cut": [{"h": "V8", "o": "V8", "c": "V8"}, {"h": "V8", "o": "V5V3", "c": "V8"}],
+    "ch": ["A5V3", "V3A3A2"],
+    "side": "V", "zs": "A", "dhS": "A", "mails": 2, "zx": "VV", "xg": "AA", "zmail": False,
+}
 
 DTY = {"aw": ("bfloat16", 2), "af": ("float32", 4), "ai": ("int32", 4), "au": ("uint16", 2), "ah": ("float16", 2)}
 _size = {k: 0 for k in DTY}
 
 
-def new(ar, n):
+def new(ar, m):
     a = _size[ar]
     step = 32 // DTY[ar][1]
-    _size[ar] = a + (n + step - 1) // step * step
-    return (ar, a, a + n, 1)
+    _size[ar] = a + (m + step - 1) // step * step
+    return (ar, a, a + m, 1)
 
 
 def sub(h, a, b, s=1):
     return (h[0], h[1] + a, h[1] + b, s)
 
 
-def ps(bank, slot, n):
-    return ("ps%d" % bank, slot * SLOT, slot * SLOT + n, 1)
+def ps(bank, slot, m=n):
+    return ("ps%d" % bank, slot * SLOT, slot * SLOT + m, 1)
 
 
 def ncol(h):
@@ -51,17 +60,26 @@ def wide(h):
     return 4 if h[0] not in DTY else DTY[h[0]][1]
 
 
-def build():
-    ops = []
-    NB = len(BLOCKS)
-    cur = [-1, 0]
+def pieces(text):
+    out, at = [], 0
+    for e, k in zip(text[::2], text[1::2]):
+        out.append((e, at, at + int(k) * n // 8))
+        at = out[-1][2]
+    return out
 
-    def add(eng, cost, reads, writes, emit, name="", kind="c", sem=None, extra=()):
-        ops.append({"e": eng, "c": cost, "r": reads, "w": writes, "f": emit, "n": name, "k": kind, "s": sem, "x": list(extra), "t": cur[0], "blk": cur[1]})
+
+def build(cfg):
+    ops = []
+    cur = [-1, 0]
+    for k in _size:
+        _size[k] = 0
+
+    def add(eng, cost, reads, writes, emit, name="", kind="c", sem=None, extra=(), grp=None):
+        ops.append({"e": eng, "c": cost, "r": reads, "w": writes, "f": emit, "n": name, "k": kind, "s": sem, "x": list(extra),
+                    "t": cur[0], "blk": cur[1], "g": grp})
         return len(ops) - 1
 
     def vts(o, i, s1, s2, op0, op1=None, name="ts"):
-        n = ncol(o)
         fast = wide(o) == 2 and wide(i) == 2
         rd = [i] + [s for s in (s1, s2) if isinstance(s, tuple)]
 
@@ -71,50 +89,65 @@ def build():
                 return q.tensor_scalar(V(o), V(i), a, None, op0)
             b = V(s2) if isinstance(s2, tuple) else s2
             return q.tensor_scalar(V(o), V(i), a, b, op0, op1)
-        return add("V", 0.03 + CY * max(64, n * (0.5 if fast else 1)), rd, [o], f, name)
+        return add("V", VO + CY * max(64, ncol(o) * (0.5 if fast else 1)), rd, [o], f, name)
 
     def vtt(o, a, b, op, name="tt"):
-        n = ncol(o)
         both = a[0] in DTY and b[0] in DTY
-        return add("V", 0.03 + CY * max(64, n * (2 if both else 1)), [a, b], [o], lambda q, V: q.tensor_tensor(V(o), V(a), V(b), op), name)
+        return add("V", VO + CY * max(64, ncol(o) * (2 if both else 1)), [a, b], [o], lambda q, V: q.tensor_tensor(V(o), V(a), V(b), op), name)
 
     def vcopy(o, i, name="cp"):
-        n = ncol(o)
         fast = wide(o) == 2 and wide(i) == 2
-        return add("V", 0.03 + CY * max(64, n * (0.5 if fast else 1)), [i], [o], lambda q, V: q.tensor_copy(V(o), V(i)), name)
+        return add("V", VO + CY * max(64, ncol(o) * (0.5 if fast else 1)), [i], [o], lambda q, V: q.tensor_copy(V(o), V(i)), name)
 
     def vset(o, v):
-        return add("V", 0.03 + CY * max(64, ncol(o) * (0.5 if wide(o) == 2 else 1)), [], [o], lambda q, V: q.memset(V(o), v), "set")
+        return add("V", VO + CY * max(64, ncol(o) * (0.5 if wide(o) == 2 else 1)), [], [o], lambda q, V: q.memset(V(o), v), "set")
+
+    def scan(o, a, b, op0, op1, name):
+        return add("V", VO + CY * max(64, ncol(o) / 2), [a, b], [o], lambda q, V: q.tensor_tensor_scan(V(o), V(a), V(b), 0.0, op0, op1), name)
 
     def act(o, i, fn, scale=1.0, bias=0.0, acc=None, name="act"):
         def f(q, V):
             if acc is None:
                 return q.activation(V(o), V(i), fn, bias, scale)
             return q.activation(V(o), V(i), fn, bias, scale, accum_out=V(acc))
-        return add("A", 0.06 + CY * ncol(o), [i], [o] + ([acc] if acc else []), f, name)
+        return add("A", AO + CY * max(64, ncol(o)), [i], [o] + ([acc] if acc else []), f, name)
 
-    def gath(eng, o, win, off, minus=None, op=None, name="gather"):
-        n = ncol(o)
+    def asel(o, i, pat, cmp, base, cm, name="asel"):
+        return add("G", 0.17 + 2 * CY * ncol(o), [i], [o], lambda q, V: q.affine_select(V(o), V(i), pat, cmp, 0.0, base, cm), name)
+
+    def iota(o, pat, base, cm):
+        return add("G", 0.13 + 2 * CY * ncol(o), [], [o], lambda q, V: q.iota(V(o), pat, base, cm), "iota")
+
+    def copy(eng, o, i, name):
         if eng == "A":
-            return add("A", 0.07 + CY * GR * n, [win, off], [o],
-                       lambda q, V: q.activation(V(o), V(win).indirect(V(off)), AF.Copy), name)
-        if minus is None:
-            return add("V", 0.05 + CY * GR * n, [win, off], [o],
-                       lambda q, V: q.tensor_copy(V(o), V(win).indirect(V(off))), name)
-        return add("V", 0.05 + CY * GR * n, [win, off, minus], [o],
-                   lambda q, V: q.tensor_tensor(V(o), V(win).indirect(V(off)), V(minus), op), name)
+            return act(o, i, AF.Copy, name=name)
+        if eng == "G":
+            return asel(o, i, [[0, ncol(o)]], OP.is_ge, 0, 0, name)
+        return vcopy(o, i, name)
 
-    def pe(o, terms, name="pe", first=True, stop=True, extra=()):
+    def gath(eng, o, win, off, other=None, op=None, name="gather"):
+        m = ncol(o)
+        if eng == "A":
+            return add("A", 0.065 + CY * GR * m, [win, off], [o],
+                       lambda q, V: q.activation(V(o), V(win).indirect(V(off)), AF.Copy), name)
+        if other is None:
+            return add("V", 0.05 + CY * GR * m, [win, off], [o],
+                       lambda q, V: q.tensor_copy(V(o), V(win).indirect(V(off))), name)
+        return add("V", 0.05 + CY * GR * m, [win, off, other], [o],
+                   lambda q, V: q.tensor_tensor(V(o), V(win).indirect(V(off)), V(other), op), name)
+
+    def pe(o, terms, name="pe", first=True, stop=True):
+        terms = [(x[0], x[1], x[2] if len(x) > 2 else o) for x in terms]
         c = 0.03
-        for l, r in terms:
-            c += PEO + PECY * max(64, ncol(r)) * (4 if l[0] == "af" else 1)
+        for l, r, _o in terms:
+            c += PEO + PECY * max(min(64, ncol(l)), ncol(r)) * (4 if l[0] == "af" else 1)
 
         def f(q, V):
             last = None
-            for k, (l, r) in enumerate(terms):
-                last = q.matmul(V(o), V(l), V(r), first and k == 0, stop and k == len(terms) - 1)
+            for k, (l, r, out) in enumerate(terms):
+                last = q.matmul(V(out), V(l), V(r), first and k == 0, stop and k == len(terms) - 1)
             return last
-        return add("P", c, [x for t in terms for x in t], [o], f, name, extra=[i for i in extra if i is not None])
+        return add("P", c, [x for t in terms for x in t[:2]], sorted({t[2] for t in terms}), f, name, grp=(terms[0][2][0], first, stop))
 
     def mailto(src, land, nm, t, b):
         sem = "%s%d_%d" % (nm, t, b)
@@ -122,185 +155,192 @@ def build():
         add("N", NETT, [], [land], None, nm, "net", sem, (k,))
 
     X = new("aw", W)
-    xin, zin, win_ = X, new("aw", NP), new("aw", 1)
+    zin, win_ = new("aw", NP), new("aw", 1)
     bain, bbin = new("ai", NP), new("ai", NP)
-    for k, (nm, h, q) in enumerate((("ba", bain, "S"), ("bb", bbin, "S"), ("zp", zin, "S"), ("wl", win_, "S"), ("xt", X, "S"))):
-        add(q, 0.1, [], [h], lambda q, V, nm=nm, h=h: q.dma_start(V(h), V(nm)), "ld" + nm, "dma", "ld" + nm)
+    for nm, h in (("ba", bain), ("bb", bbin), ("zp", zin), ("wl", win_), ("xt", X)):
+        add("S", 0.1, [], [h], lambda q, V, nm=nm, h=h: q.dma_start(V(h), V(nm)), "ld" + nm, "dma", "ld" + nm)
 
     ONE = new("aw", 128)
-    ID, NEG, BO, LT, L64, L4, T1 = [new("aw", 128) for _ in range(7)]
-    MID = {v: new("aw", 128) for v in (-64, -2, 4, 2048, -4096, 528384, -2 ** 23, 2 ** 30, 65536, 98304)}
+    ID, BO, BN, LT, T1, LS, LQ, WB = [new("aw", 128) for _ in range(8)]
+    MID = {v: new("aw", 128) for v in (-1, 0.5, -0.5, 1.25, 32, -32, -64, -128, 145, SEG, BIG, 2 * BIG, 0.5 / BIG, -4096,
+                                       -2.0 ** -10, -2.0 ** -17, 2.0 ** -30)}
+    HID = {v: new("ah", 128) for v in (1, -1, 0.5, 32, 2080, 3232, 2.0 ** -12, -2.0 ** -12)}
+    FID = {v: new("af", 128) for v in (1, 0.5, 2.0 ** -12)}
+    HALF = new("af", 128)
+    G1, G2, GM = new("aw", 8), new("aw", 8), new("aw", 8)
     D, WD = new("aw", 144), new("aw", 144)
-    WB, WB64 = new("aw", 128), new("aw", 128)
-    HI, H65, H101, H32, HH = [new("ah", 128) for _ in range(5)]
-    MONE = new("aw", max(BLOCKS))
-    IF = new("af", 128)
-    NCM = max(BLOCKS) // 16
-    MASK = new("aw", 16 * max(BLOCKS))
+    ZERO, CONST = new("aw", n), new("aw", 5 * n)
+    MASK = new("aw", 16 * n)
+    NEG, HI = MID[-1], HID[1]
 
-    def asel(o, i, pat, cmp, base, cm):
-        return add("G", 0.4, [i], [o], lambda q, V: q.affine_select(V(o), V(i), pat, cmp, 0.0, base, cm), "asel")
     vset(ONE, 1.0)
     asel(ID, ONE, [[-1, 128]], OP.is_equal, 0, 1)
     asel(T1, ONE, [[-16, 8], [0, 16]], OP.is_ge, 0, 1)
     asel(BO, T1, [[16, 8], [0, 16]], OP.is_ge, 15, -1)
     asel(LT, BO, [[1, 128]], OP.is_gt, 0, -1)
-    B1, B2, BASE = new("ai", NCM), new("ai", NCM), new("ai", NCM)
-    add("G", 0.2, [], [B1], lambda q, V: q.iota(V(B1), [[0, NCM]], 0, 16), "iota")
-    add("G", 0.2, [], [B2], lambda q, V: q.iota(V(B2), [[256, NCM]], 0, 0), "iota")
-    vts(B1, B1, 255, None, OP.bitwise_and)
-    vtt(BASE, B1, B2, OP.add)
-    vcopy(HI, ID)
-    vts(H65, ID, 2080.0, None, OP.mult)
-    vts(H101, ID, 3232.0, None, OP.mult)
-    vts(H32, ID, 32.0, None, OP.mult)
-    vts(NEG, ID, -1.0, None, OP.mult)
+    for v in sorted(HID):
+        vts(HID[v], ID, float(v), None, OP.mult)
     for v in sorted(MID):
         act(MID[v], ID, AF.Copy, scale=float(v))
-    act(IF, ID, AF.Copy)
-    vtt(L64, LT, MID[-64], OP.add)
-    vtt(L4, LT, MID[4], OP.add)
+    for v in sorted(FID):
+        act(FID[v], ID, AF.Copy, scale=float(v))
+    vset(HALF, -0.5)
+    act(LS, LT, AF.Copy, scale=2.0 ** -18)
+    act(T1, ID, AF.Copy, scale=-2.0 ** -19)
+    vtt(LQ, LS, T1, OP.add)
+    act(BN, BO, AF.Copy, scale=-1.0)
+    for h, v in ((G1, 1.0), (G2, 2.0 / BIG), (GM, -1.0 / BIG)):
+        vts(h, sub(BO, 0, 128, 16), v, None, OP.mult)
     vset(D, 0.0)
     vcopy(sub(D, 15, 143, 16), sub(BO, 0, 128, 16))
     WF = new("af", 1)
     vcopy(WF, win_)
     vts(WD, D, WF, None, OP.mult)
     vts(WB, BO, WF, None, OP.mult)
-    vts(WB64, WB, 2048.0, None, OP.mult)
-    vset(MONE, -1.0)
-    vts(HH, ID, 0.5, None, OP.mult)
-    vset(MASK, 1.0)
-    vset(sub(MASK, 0, 16 * max(BLOCKS), 16), 0.0)
+    vset(ZERO, 0.0)
 
-    p0 = [sum(BLOCKS[:b]) for b in range(NB)]
+    def part(k):
+        return sub(CONST, k * n, (k + 1) * n)
+    for k, v in enumerate((129.0 * 4096, 65536.0 - 2.0 ** 23, 2048.0 - BIG, 113.0, 103.0)):
+        vset(part(k), v)
+    vset(MASK, 1.0)
+    vset(sub(MASK, 0, 16 * n, 16), 0.0)
+    B1, B2, BASE = new("ai", n // 16), new("ai", n // 16), new("ai", n // 16)
+    iota(B1, [[0, n // 16]], 0, 16)
+    iota(B2, [[256, n // 16]], 0, 0)
+    vts(B1, B1, 255, None, OP.bitwise_and)
+    vtt(BASE, B1, B2, OP.add)
+    J, JF, J0 = new("ai", 1), new("af", 1), new("af", 1)
+    I1, I2, PLACE = new("ai", n), new("ai", n), new("ah", n)
+    F1, F2 = new("af", n), new("af", n)
+    iota(J, [[0, 1]], 0, 1)
+    iota(I1, [[16, n]], n - 1024, 0)
+    iota(I2, [[15, n]], n, 0)
+    vts(J, J, 15, None, OP.bitwise_and)
+    vcopy(JF, J)
+    vts(J0, JF, 0.0, None, OP.is_equal)
+    vts(F1, I1, JF, None, OP.add)
+    vts(F2, I2, J0, None, OP.mult)
+    vtt(PLACE, F1, F2, OP.subtract)
+
     big = []
+    ZS = new("aw", 16 * n)
+    vset(ZS, 0.0)
     for b in range(NB):
-        n = BLOCKS[b]
-        d = {k: new("aw", 16 * n) for k in ("h", "o", "c", "ch", "ah", "zx", "zs")}
-        d.update({k: new("aw", n) for k in ("live", "rec", "want", "am", "sv", "jk", "ry", "ay", "spl", "fl", "so", "fu")})
-        d.update({k: new("ah", n) for k in ("Hc", "Oc", "Cc", "tO", "tC", "tH", "s1", "s2")})
-        d.update({k: new("af", n) for k in ("dhS", "m", "gl", "dhG", "m2", "stU", "xg", "P", "pU")})
+        d = {k: new("aw", 16 * n) for k in ("mh", "mo", "mc", "ch", "mx", "zx")}
+        d["zs"] = ZS
+        d["win"] = new("aw", 3 * SEG)
+        d.update({k: new("aw", n) for k in ("st", "rec", "want", "cnt", "am", "sv", "spl", "low", "x", "fl", "so", "fu", "g1", "g2")})
+        d["ar"], d["yes"], d["p1"] = new("aw", 2 * n), new("aw", 8), new("af", 2 * n)
+        d.update({k: new("ah", n) for k in ("Hc", "Oc", "Cc", "stK")})
+        d.update({k: new("af", n) for k in ("dhS", "m", "mw", "xg", "P", "pU", "p2", "A")})
         d.update({k: new("ai", n) for k in ("T", "C", "TU", "xf")})
         d.update({k: new("ai", n // 16) for k in ("ui", "ua", "ul")})
         d["C16"], d["ch16"], d["l16"] = new("au", n), new("au", n), new("au", n // 16)
-        vset(d["zs"], 0.0)
         big.append(d)
-    ACC = new("af", 16 * NREAD)
-    RM = [[new("aw", 128) for _ in range(NB)] for _ in range(2)] * 3
-    subn = [0]
-    lastv = [None]
+    ACC = [new("af", 2) for _ in range(NREAD)]
+    KC = [new("af", 1) for _ in range(NREAD)]
+    KJ = new("af", 2)
 
     mail = []
     for b in range(NB):
-        n = BLOCKS[b]
-        A16, B16, I0, G0 = new("au", n), new("au", n), new("aw", n), new("aw", n)
-        vcopy(A16, sub(bain, p0[b], p0[b] + n))
-        vcopy(B16, sub(bbin, p0[b], p0[b] + n))
-        vset(I0, 0.0)
-        vset(G0, 0.0)
-        mail.append((A16, B16, sub(zin, p0[b], p0[b] + n), I0, G0))
+        A16, B16 = new("au", n), new("au", n)
+        vcopy(A16, sub(bain, n * b, n * b + n))
+        vcopy(B16, sub(bbin, n * b, n * b + n))
+        mail.append((A16, B16, sub(zin, n * b, n * b + n), ONE, None, ONE))
 
     for t in range(NREAD):
         last = t == NREAD - 1
         nxt = []
         for b in range(NB):
             cur[0], cur[1] = t, b
-            n, d, par = BLOCKS[b], big[b], b & 1
-            H16, O16, z, I, G = mail[b][t & 1], mail[b][1 - (t & 1)], mail[b][2], mail[b][3], mail[b][4]
-            hp, lin = ps(2, 2 * par, n), ps(2, 2 * par + 1, n)
-            sg = ps(3 + par, 3, n)
+            d = big[b]
+            Bd, Bv, Bx, By = b, 2 + b, 4 + b, 6 + b
+            H16, O16, z, R = mail[b][t & 1], mail[b][1 - (t & 1)], mail[b][2], mail[b][5]
+            hp, lin, zp, sel = [ps(Bx, k) for k in range(4)]
             vts(d["Hc"], H16, -2048.0, None, OP.add, name="Hc")
             vts(d["Oc"], O16, -2048.0, None, OP.add, name="Oc")
+            pe(zp, [(ID, z)], "zPS")
             pe(hp, [(HI, d["Hc"])], "HcPS")
-            pe(lin, [(H65, d["Hc"]), (H101, d["Oc"])], "lin")
+            pe(lin, [(HID[2080], d["Hc"]), (HID[3232], d["Oc"])], "lin")
             vtt(d["P"], d["Oc"], hp, OP.mult, "P")
             vtt(d["T"], d["P"], lin, OP.add, "T")
             vts(d["C"], d["T"], 5, 4095, OP.arith_shift_right, OP.bitwise_and, name="C")
             vcopy(d["C16"], d["C"], "C16")
             vts(d["Cc"], d["C16"], -2048.0, None, OP.add, name="Cc")
-            vtt(d["live"], d["Oc"], hp, OP.not_equal, "live")
-            act(sub(d["zs"], 0, 16 * n, 16), z, AF.Copy, name="zs")
-            mk = sub(MASK, 0, 16 * n)
-            add("V", 0.03 + CY * 8 * n, [mk, d["zs"]], [d["zx"]],
-                lambda q, V, mk=mk, d=d: q.tensor_tensor_scan(V(d["zx"]), V(mk), V(d["zs"]), 0.0, OP.mult, OP.add), "zx")
-            act(sg, G, AF.Sign, scale=-1.0, bias=1.5, name="sg")
-            vtt(d["gl"], d["live"], sg, OP.mult, "gl")
-        for b in range(NB):
-            cur[0], cur[1] = t, b
-            n, d, par = BLOCKS[b], big[b], b & 1
-            H16, O16, z, I, G = mail[b][t & 1], mail[b][1 - (t & 1)], mail[b][2], mail[b][3], mail[b][4]
-            dh, do, dc, cap = [ps(3 + par, k, n) for k in range(4)]
-            vs = ps(5, b, n)
-            pc = [(k * n // PIECES, (k + 1) * n // PIECES) for k in range(PIECES)]
-            for k, lst, dist in (("h", H16, dh), ("o", O16, do), ("c", d["C16"], dc)):
-                res = d["ah"] if k == "h" else d[k]
-                for (q0, q1), mode in zip(pc, MODE[b][k]):
-                    e0, e1 = 16 * q0, 16 * q1
-                    if mode == "F":
-                        gath("V", sub(d[k], e0, e1), X, sub(lst, q0, q1), sub(d["zx"], e0, e1), OP.subtract, k)
-                        act(sub(res, e0, e1), sub(d[k], e0, e1), AF.Abs, name="abs" + k)
-                        continue
-                    gath(mode, sub(d[k], e0, e1), X, sub(lst, q0, q1), name=k)
-                    for a0 in range(e0, e1, 512):
-                        a1 = min(a0 + 512, e1)
-                        tile = ("ps%d" % (subn[0] & 1), 0, a1 - a0, 1)
-                        subn[0] += 1
-                        pe(tile, [(ID, sub(d[k], a0, a1)), (NEG, sub(d["zx"], a0, a1))], "sub")
-                        act(sub(res, a0, a1), tile, AF.Abs, name="abs" + k)
-                for q0, q1 in (pc if k in SPLIT else [(0, n)]):
-                    pe(sub(dist, q0, q1), [(sub(D, 15 - j, 143 - j), sub(res, 16 * q0 + j, 16 * q1, 16)) for j in range(16)], "d" + k)
+            vtt(d["st"], d["Oc"], hp, OP.is_equal, "st")
+            if cfg["zx"][b] == "G":
+                for j in range(16):
+                    copy("G", sub(d["zx"], j, 16 * n, 16), z, "zx")
+            else:
+                copy(cfg["zs"], sub(d["zs"], 0, 16 * n, 16), z, "zs")
+                scan(d["zx"], MASK, d["zs"], OP.mult, OP.add, "zx")
+            dh, do, dc = ps(Bd, 0), ps(Bd, 1), ps(By, 2)
+            vs, dp = ps(Bv, 0), ps(By, 1)
+            for k, lst, dist in (("h", H16, dh), ("c", d["C16"], dc), ("o", O16, do)):
+                at = SEG * "hoc".index(k)
+                side, col, res = sub(d["win"], at, at + n), sub(d["win"], at + n, at + SEG), d["m" + k]
+                for e, q0, q1 in pieces(cfg["col"][b][k]):
+                    gath(e, sub(col, 16 * q0, 16 * q1), X, sub(lst, q0, q1), name=k)
+                for _e, q0, q1 in pieces(cfg["cut"][b][k]):
+                    head = sub(col, 16 * q0, 16 * q1, 16)
+                    copy(cfg["side"], sub(side, q0, q1), head, "side" + k)
+                    vtt(head, head, sub(zp, q0, q1), OP.max, "fix" + k)
+                    scan(sub(res, 16 * q0, 16 * q1), sub(d["zx"], 16 * q0, 16 * q1), sub(col, 16 * q0, 16 * q1), OP.min, OP.max, "max" + k)
+                raw = [side] + [sub(col, j, 16 * n, 16) for j in range(1, 16)]
+                opening = (d["st"], MID[0.5 / BIG], dist) if k == "o" else (ID, ZERO, dist)
+                pe(None, [opening] + [(raw[j], GM, sub(dist, j, n, 16)) for j in range(1, 16)], "raw" + k, stop=False)
+                pe(None, [(side, GM, sub(dist, 0, n, 16))] + [(sub(res, j, 16 * n, 16), G2, sub(dist, j, n, 16)) for j in range(16)], "d" + k, first=False)
                 if k == "h":
-                    for j0 in range(0, 16, VH):
-                        terms = [(NEG, sub(d["h"], j, 16 * n, 16)) for j in range(j0, j0 + VH)]
-                        pe(vs, terms, "voteh", first=j0 == 0, stop=False, extra=lastv)
-            act(d["dhS"], dh, AF.Copy, name="dhS")
-            vtt(d["dhG"], d["gl"], dh, OP.mult, "dhG")
-            vtt(d["m2"], d["dhG"], do, OP.min, "m2")
-            vtt(d["m"], d["dhS"], dc, OP.min, "m")
-            vtt(d["want"], d["m2"], dc, OP.is_gt, "want")
+                    pe(vs, [(NEG, raw[j]) for j in range(8)], "voteh", stop=False)
+                    pe(vs, [(NEG, raw[j]) for j in range(8, 16)], "voteh", first=False, stop=False)
+                    copy(cfg["dhS"], d["dhS"], dh, "dhS")
+
+                if k == "c":
+                    vtt(d["x"], d["dhS"], dc, OP.is_le, "x")
+                    vtt(d["m"], d["dhS"], dc, OP.min, "m")
+                    pe(dp, [(R, MID[2.0 ** -30]), (d["st"], ID), (ID, d["x"])], "pen")
+                    vtt(d["mw"], d["m"], dp, OP.max, "mw")
+            cap = ps(By, 0)
+            vtt(d["want"], d["mw"], do, OP.is_lt, "want")
             vtt(d["rec"], d["m"], do, OP.is_ge, "rec")
-            pe(cap, [(L64, d["want"])], "cap")
-            vts(d["am"], cap, -60.0, None, OP.is_lt, name="am")
-            rp, ap_, sp_, cs = dh, do, dc, cap
-            pe(rp, [(ID, d["rec"])], "recPS")
-            vtt(d["tO"], d["Oc"], rp, OP.mult, "tO")
-            pe(ap_, [(ID, d["am"])], "amPS")
-            pe(sp_, [(ID, sub(ONE, 0, n)), (NEG, d["rec"]), (NEG, d["am"])], "sH")
-            vtt(d["tC"], d["Cc"], ap_, OP.mult, "tC")
-            vtt(d["tH"], d["Hc"], sp_, OP.mult, "tH")
-            pe(cs, [(HI, d["tO"]), (HI, d["tC"]), (HI, d["tH"])], "chS")
-            vts(d["ch16"], cs, 2048.0, None, OP.add, name="ch16")
-            for (q0, q1), e in zip(pc, CHQ[b]):
-                gath(e, sub(d["ch"], 16 * q0, 16 * q1), X, sub(d["ch16"], q0, q1), name="ch")
-            lastv[0] = pe(vs, [(ID, sub(d["ch"], j, 16 * n, 16)) for j in range(16)], "vote", first=False)
+            scan(d["cnt"], sub(MASK, 0, n), d["want"], OP.mult, OP.add, "cntw")
+            pe(sel, [(HI, PLACE), (d["rec"], MID[SEG])], "sel", stop=False)
+            pe(cap, [(d["want"], MID[-64]), (d["cnt"], ID)], "cap")
+            act(d["am"], cap, AF.Sign, scale=-1.0, bias=-59.5, name="am")
+            pe(sel, [(MID[SEG], d["am"])], "sel2", first=False)
+            vts(d["ch16"], sel, 1024.0 + SEG, None, OP.add, name="ch16")
+            for e, q0, q1 in pieces(cfg["ch"][b]):
+                gath(e, sub(d["ch"], 16 * q0, 16 * q1), d["win"], sub(d["ch16"], q0, q1), name="ch")
+                scan(sub(d["mx"], 16 * q0, 16 * q1), sub(MASK, 0, 16 * (q1 - q0)), sub(d["ch"], 16 * q0, 16 * q1), OP.mult, OP.max, "mx")
+            for q0 in (0, n // 2):
+                pe(sub(vs, q0, q0 + n // 2), [(ID, sub(d["ch"], 16 * q0 + j, 16 * q0 + 8 * n, 16)) for j in range(16)], "vote", first=False, stop=q0 > 0)
         for b in range(NB):
             cur[0], cur[1] = t, b
-            n, d, par = BLOCKS[b], big[b], b & 1
-            z = mail[b][2]
-            mx = d["zx"]
-            for k in range(PIECES):
-                q0, q1 = 16 * (k * n // PIECES), 16 * ((k + 1) * n // PIECES)
-                mk, cp, mp = sub(MASK, 0, q1 - q0), sub(d["ch"], q0, q1), sub(mx, q0, q1)
-                add("V", VO + CY * (q1 - q0) / 2, [mk, cp], [mp],
-                    lambda q, V, mk=mk, cp=cp, mp=mp: q.tensor_tensor_scan(V(mp), V(mk), V(cp), 0.0, OP.mult, OP.max), "mx")
-            M = sub(mx, 15, 16 * n, 16)
-            ur, uc = ps(6, 2 * par, n), ps(6, 2 * par + 1, n)
-            d["M"], d["ur"], d["uc"] = M, ur, uc
+            d = big[b]
+            Bd, Bv, Bx, By = b, 2 + b, 4 + b, 6 + b
+            M = sub(d["mx"], 15, 16 * n, 16)
             out = {}
             if not last:
                 out["AB"] = new("au", 2 * n)
-                out["ZIG"] = new("aw", 3 * n)
+                out["ZIG"] = new("aw", 4 * n)
                 out["A"], out["B"] = sub(out["AB"], 0, n), sub(out["AB"], n, 2 * n)
-                out["z"], out["I"], out["G"] = [sub(out["ZIG"], k * n, (k + 1) * n) for k in range(3)]
-                ulp = sub(uc, 0, n // 16)
-                pe(ulp, [(sub(WD, 15 - j, 143 - j), sub(mx, 15 + 16 * j, 16 * n, 256)) for j in range(16)], "ulist")
+                out["z"], out["I"], out["S"], out["G"] = [sub(out["ZIG"], k * n, (k + 1) * n) for k in range(4)]
+                ulp = ps(Bx, 3, n // 16)
+                pe(ulp, [(sub(WD, 15 - j, 143 - j), sub(d["mx"], 15 + 16 * j, 16 * n, 256)) for j in range(16)], "ulist")
                 vcopy(d["ui"], ulp, "ui")
                 vts(d["ua"], d["ui"], 15, None, OP.bitwise_and, name="ua")
-                vtt(d["ul"], d["ua"], sub(BASE, 0, n // 16), OP.add, "ul")
+                vtt(d["ul"], d["ua"], BASE, OP.add, "ul")
                 vcopy(d["l16"], d["ul"], "l16")
-                xw = sub(X, 16 * p0[b], 16 * (p0[b] + n))
-                gath("V", d["xg"], xw, d["l16"], M, OP.add, "xg")
-                vts(d["xf"], d["xg"], -0.5, 0.5, OP.add, OP.mult, name="xf")
+                xw = sub(X, 16 * n * b, 16 * n * (b + 1))
+                if cfg["xg"][b] == "V":
+                    gath("V", d["xg"], xw, d["l16"], M, OP.add, "xg")
+                    vts(d["xf"], d["xg"], -0.5, 0.5, OP.add, OP.mult, name="xf")
+                else:
+                    pe(ps(Bx, 0), [(MID[0.5], M)], "Mh")
+                    add("A", 0.065 + CY * GR * n, [xw, d["l16"]], [d["xg"]],
+                        lambda q, V, d=d, xw=xw: q.activation(V(d["xg"]), V(xw).indirect(V(d["l16"])), AF.Copy, -0.25, 0.5), "xg")
+                    vtt(d["xf"], d["xg"], ps(Bx, 0), OP.add, "xf")
                 add("V", 0.05 + CY * 3.8 * n, [d["xf"], d["l16"]], [xw],
                     lambda q, V, d=d, xw=xw: q.tensor_copy(V(xw).indirect(V(d["l16"])), V(d["xf"])), "scat")
             else:
@@ -308,88 +348,117 @@ def build():
             d["out"] = out
         for b in range(NB):
             cur[0], cur[1] = t, b
-            n, d, par = BLOCKS[b], big[b], b & 1
-            H16, O16, z, I, G = mail[b][t & 1], mail[b][1 - (t & 1)], mail[b][2], mail[b][3], mail[b][4]
-            out, M, ur, uc = d["out"], d["M"], d["ur"], d["uc"]
-            one = sub(ONE, 0, n)
-            S0, S1, S2, S3 = [ps(3 + par, k, n) for k in range(4)]
-            vs, cn = ps(5, b, n), S3
-            old0, old1 = ps(2, 2 * par, n), ps(2, 2 * par + 1, n)
-            yes, nm = ps(7, 2 * par, n), ps(7, 2 * par + 1, n)
+            d = big[b]
+            Bd, Bv, Bx, By = b, 2 + b, 4 + b, 6 + b
+            z, low0, spl0, R = mail[b][2:6]
+            out, M = d["out"], sub(d["mx"], 15, 16 * n, 16)
+            Hc, Oc, Cc, st = d["Hc"], d["Oc"], d["Cc"], d["st"]
+            ay, ry = sub(d["ar"], 0, n), sub(d["ar"], n, 2 * n)
+            Bt, Lt, DC, DO = [ps(Bd, k) for k in range(4)]
+            ur, zd, Ht = ps(Bx, 1), ps(Bx, 2), ps(Bx, 3)
+            vs, ct, y, par = ps(Bv, 0), ps(Bv, 1, 8), ps(Bv, 2), ps(Bv, 3)
+            Rt, At, st_ = ps(By, 0), ps(By, 2), ps(By, 3)
+            pe(DC, [(HI, Cc), (HID[-1], Hc)], "DC")
+            pe(DO, [(HI, Oc), (HID[-1], Hc)], "DO")
+            pe(At, [(ID, part(2)), (HI, Hc), (MID[BIG], st)], "At")
+            spl, low = (d["spl"], d["low"]) if last else (out["S"], out["I"])
+            pe(st_, [(MID[-64], low0), (MID[-128], st), (d["rec"], MID[-64]), (MID[-32], d["am"])]
+               + ([(MID[-2.0 ** -10], spl0)] if t > 0 else []), "splt", stop=False)
             act(d["sv"], vs, AF.Sign, bias=0.5, name="sv")
-            pe(cn, [(BO, d["sv"])], "cnt")
-            acc = sub(ACC, 16 * t + b, 16 * t + b + 1)
-            act(yes, cn, AF.Sign, bias=0.5, acc=None if last else acc, name="yes")
-            if not last:
-                rm = RM[t][b]
-                add("A", 0.06 + CY * 128, [ONE, acc], [rm], lambda q, V, rm=rm, acc=acc: q.activation(V(rm), V(ONE), AF.Copy, 0.0, V(acc)), "RM")
-                pe(old1, [(ID, z), (NEG, M)], "zd")
-                act(out["z"], old1, AF.Abs, name="z")
-            vtt(d["ry"], d["rec"], yes, OP.is_equal, "ry")
-            vtt(d["ay"], d["am"], yes, OP.is_equal, "ay")
-            pe(old0, [(ID, G), (ID, d["ay"])], "Gs")
-            act(out["G"], old0, AF.Copy, name="G")
-            pe(S0, [(ID, d["ry"]), (ID, d["ay"])], "mv")
-            vtt(nm, d["live"], S0, OP.is_gt, "nm")
-            vtt(out["I"], I, nm, OP.not_equal, "I")
-            vtt(d["spl"], I, nm, OP.mult, "spl")
-            if not last:
-                zl, lh, lo = new("aw", 3 * n), new("au", n), new("au", n)
-                mailto(out["ZIG"], zl, "rz", t, b)
-            pe(S1, [(LT, d["spl"])], "bef")
-            act(d["fl"], S1, AF.Copy, scale=0.5, bias=128.75, name="fl")
-            pe(S2, [(L4, d["spl"]), (MID[-2], d["fl"])], "par")
-            vts(d["so"], S2, -253.5, None, OP.is_gt, name="so")
-            pe(S3, [(ID, one), (NEG, d["ry"]), (NEG, d["ay"]), (NEG, d["so"])], "sH2")
-            pe(S0, [(ID, d["ay"]), (ID, d["so"])], "a2")
-            vtt(d["s1"], d["tO"], yes, OP.mult, "tO2")
-            vtt(d["tC"], d["Cc"], S0, OP.mult, "tC2")
-            vtt(d["tH"], d["Hc"], S3, OP.mult, "tH2")
-            pe(S1, [(HH, d["tO"]), (HH, d["s1"]), (HI, d["tC"]), (HI, d["tH"])], "nHs")
-            oh, oo = (out["A"], out["B"]) if t % 2 == 0 else (out["B"], out["A"])
-            vts(oh, S1, 2048.0, None, OP.add, name="nH")
-            if not last:
-                mailto(oh, lh, "rh", t, b)
+            pe(st_, [(BN, d["sv"])], "splt", first=False)
+            vts(spl, st_, 33.0, 2.0 ** 17, OP.is_gt, OP.mult, name="spl")
+            act(low, st_, AF.Sign, scale=-1.0, bias=-94.5, name="low")
+            pe(None, [(BO, d["sv"], ps(By, 0)), (MID[32], d["am"], ps(By, 0))], "ayt")
+            pe(None, [(BO, d["sv"], ps(By, 1)), (d["rec"], MID[32], ps(By, 1))], "ryt")
+            act(d["ar"], ps(By, 0, 2 * n), AF.Sign, bias=-31.0, name="ar")
+            if t > 0:
+                vts(d["stK"], st, KC[t - 1], None, OP.mult, name="stK")
+            pe(None, [(ID, sub(CONST, 0, 2 * n), ps(Bd, 0, 2 * n)), (HID[32], Oc, Lt)]
+               + ([(HID[32], d["stK"], Lt)] if t > 0 else []), "g2", stop=False)
             pe(ur, [(WB, M)], "uraw")
             act(d["fu"], ur, AF.Copy, scale=1.0 / 4096, bias=128.5 + 1.0 / 8192, name="fu")
-            pe(uc, [(MID[528384], one), (MID[-4096], d["fu"]), (WB, M)], "u")
-            lin = [(WB64, M), (MID[-2 ** 23], d["fu"]), (MID[2 ** 30], one), (H32, d["Hc"]), (MID[98304 if t else 65536], one)]
-            if t > 0:
-                lin += [(RM[t - 1][k], sub(MONE, 0, n)) for k in range(NB)]
-            vtt(d["pU"], d["Hc"], uc, OP.mult, "pU")
-            pe(ur, lin, "linU")
-            vtt(d["TU"], d["pU"], ur, OP.add, "TU")
-            vts(d["TU"], d["TU"], 5, 4095, OP.arith_shift_right, OP.bitwise_and, name="U")
-            pe(S3, [(ID, d["live"]), (NEG, d["spl"])], "sO")
-            pe(S0, [(ID, one), (NEG, d["live"])], "st")
-            vtt(d["stU"], d["TU"], S0, OP.mult, "stU")
-            vtt(d["s2"], d["Oc"], S3, OP.mult, "s2")
-            vtt(d["s1"], d["spl"], S1, OP.mult, "s1")
-            pe(S2, [(MID[2048], d["live"]), (IF, d["stU"]), (HI, d["s2"]), (HI, d["s1"])], "nOs")
-            vcopy(oo, S2, "nO")
+            pe(Bt, [(MID[-4096], d["fu"]), (WB, M), (HID[-2.0 ** -12], Oc), (HID[2.0 ** -12], Hc)], "u", first=False, stop=False)
             if not last:
-                mailto(oo, lo, "ro", t, b)
-                nxt.append(((lh, lo) if t % 2 == 0 else (lo, lh)) + (sub(zl, 0, n), sub(zl, n, 2 * n), sub(zl, 2 * n, 3 * n)))
+                pe(zd, [(ID, z), (NEG, M)], "zd")
+                act(out["z"], zd, AF.Abs, name="z")
+                pe(ct, [(d["sv"], G1)], "ct")
+                act(d["yes"], ct, AF.Sign, bias=0.5, acc=sub(ACC[t], b, b + 1), name="yes")
+                if b == NB - 1:
+                    kt = ps(Bv, 1, NB)
+                    pe(kt, [(HALF, ACC[t])], "kt")
+                    act(KJ, kt, AF.Copy, bias=4.0 * n, acc=KC[t], name="K")
+            pe(par, [(MID[1.25], part(4)), (LQ, spl)], "par")
+            vtt(d["p1"], d["ar"], ps(Bd, 2, 2 * n), OP.mult, "p1")
+            pe(Ht, [(HID[0.5], Cc), (HID[0.5], Oc), (FID[0.5], sub(d["p1"], 0, n)), (FID[0.5], sub(d["p1"], n, 2 * n))], "H1", stop=False)
+            if not last:
+                pe(Rt, [(MID[145], part(3)), (MID[2 * BIG], ay)], "Rt")
+                vtt(out["G"], R, Rt, OP.mult, "G")
+                zl, la = new("aw", 4 * n), new("au", 2 * n)
+                if cfg["zmail"]:
+                    mailto(out["z"], sub(zl, 0, n), "rq", t, b)
+                    mailto(sub(out["ZIG"], n, 4 * n), sub(zl, n, 4 * n), "rz", t, b)
+                else:
+                    mailto(out["ZIG"], zl, "rz", t, b)
+            else:
+                pe(y, [(MID[-0.5], low), (MID[-2.0 ** -17], spl)], "y")
+                act(out["I"], y, AF.Copy, bias=0.5, name="I")
+                vts(d["g1"], R, 2.0, None, OP.is_ge, name="once")
+                vts(d["g2"], R, 2.0 ** 20, None, OP.is_ge, name="twice")
+                pe(Rt, [(ID, d["g1"]), (ID, d["g2"]), (MID[0.5], ay)], "Rt")
+                act(out["G"], Rt, AF.Copy, bias=0.5, name="G")
+            vtt(d["A"], spl, At, OP.max, "A")
+            act(d["fl"], par, AF.Copy, name="fl")
+            vtt(d["so"], d["fl"], par, OP.is_equal, "so")
+            vtt(d["p2"], d["so"], DC, OP.mult, "p2")
+            pe(Bt, [(FID[2.0 ** -12], d["p2"])], "B2", first=False)
+            pe(Ht, [(FID[1], d["p2"])], "H2", first=False)
+            oh, oo = (out["A"], out["B"]) if t % 2 == 0 else (out["B"], out["A"])
+            vtt(d["pU"], d["A"], Bt, OP.mult, "pU")
+            vtt(d["TU"], d["pU"], Lt, OP.add, "TU")
+            vts(oh, Ht, 2048.0, None, OP.add, name="nH")
+            la_h, la_o = [sub(la, k * n, k * n + n) for k in ((0, 1) if t % 2 == 0 else (1, 0))] if not last else (None, None)
+            if not last and cfg["mails"] == 3:
+                mailto(oh, la_h, "rh", t, b)
+            vts(d["TU"], d["TU"], 5, 4095, OP.arith_shift_right, OP.bitwise_and, name="U")
+            vcopy(oo, d["TU"], "nO")
+            if not last:
+                if cfg["mails"] == 3:
+                    mailto(oo, la_o, "ro", t, b)
+                else:
+                    mailto(out["AB"], la, "ro", t, b)
+                nxt.append((sub(la, 0, n), sub(la, n, 2 * n)) + tuple(sub(zl, k * n, k * n + n) for k in range(4)))
             else:
                 for k, nme in (("G", "yg"), ("I", "yi"), ("A", "ya"), ("B", "yb")):
-                    add("S", 0.1, [out[k]], [], lambda q, V, nme=nme, h=out[k], a=p0[b], n=n: q.dma_start(V(nme)[:, a:a + n], V(h)), "st" + nme, "dma", "st%s%d" % (nme, b))
+                    add("S", 0.1, [out[k]], [], lambda q, V, nme=nme, h=out[k], a=n * b: q.dma_start(V(nme)[:, a:a + n], V(h)), "st" + nme, "dma", "st%s%d" % (nme, b))
         mail = nxt
     return ops
 
 
 def depend(ops):
     hist = {}
+    closed, since = {}, {}
     for i, o in enumerate(ops):
         dep = set(o["x"])
         for h, w in [(h, 0) for h in o["r"]] + [(h, 1) for h in o["w"]]:
-            for j, a, b, jw in hist.get(h[0], ()):
-                if (w or jw) and a < h[2] and h[1] < b:
+            for j, a, b, jw, s in hist.get(h[0], ()):
+                if (w or jw) and a < h[2] and h[1] < b and not (s == h[3] > 1 and (a - h[1]) % s):
                     dep.add(j)
         for h, w in [(h, 0) for h in o["r"]] + [(h, 1) for h in o["w"]]:
             lst = hist.setdefault(h[0], [])
             if w:
-                lst[:] = [e for e in lst if not (h[1] <= e[1] and e[2] <= h[2] and h[3] == 1)]
-            lst.append((i, h[1], h[2], w))
+                lst[:] = [e for e in lst if not (h[1] <= e[1] and e[2] <= h[2] and (h[3] == 1 or (h[3] == e[4] and (e[1] - h[1]) % h[3] == 0)))]
+            lst.append((i, h[1], h[2], w, h[3]))
+        if o["g"]:
+            bank, first, stop = o["g"]
+            if first and bank in closed:
+                dep.add(closed[bank])
+            if first != stop or not first:
+                if first or stop:
+                    dep.update(since.get(bank, ()))
+                    since[bank] = []
+                if stop:
+                    closed[bank] = i
+            since.setdefault(bank, []).append(i)
         dep.discard(i)
         o["d"] = sorted(dep)
         o["b"] = sorted({h[0] for h in o["r"] + o["w"] if h[0] not in DTY})
@@ -398,88 +467,82 @@ def depend(ops):
 LDT = {"ldba": 3.0, "ldbb": 3.2, "ldzp": 3.4, "ldwl": 3.4, "ldxt": 7.0}
 
 
-def schedule(ops, pri, pred, succ):
-    n = len(ops)
-    left = [len(p) for p in pred]
-    ready = {}
-    est = [0.0] * n
-    free, bank = {}, {}
-    end, start = [0.0] * n, [0.0] * n
-    for i in range(n):
-        if not left[i]:
-            ready.setdefault(ops[i]["e"], []).append(i)
-    order, done = [], 0
-    while done < n:
-        best = None
-        for e, lst in ready.items():
-            if not lst:
-                continue
-            t0 = free.get(e, 0.0) if e != "N" else 0.0
-            cand = []
-            for i in lst:
-                s = max(t0, est[i])
-                for b in ops[i]["b"]:
-                    for e2, u in bank.get(b, {}).items():
-                        if e2 != e:
-                            s = max(s, u + WAKE)
-                cand.append((s, -pri[i], i))
-            s0 = min(cand)[0]
-            c = min((c for c in cand if c[0] <= s0 + WIN), key=lambda c: c[1])
-            if best is None or c[0] < best[0]:
-                best = (c[0], c[2], e)
-        s, i, e = best
-        ready[e].remove(i)
-        o = ops[i]
-        start[i] = s
-        end[i] = s + o["c"]
-        fin = end[i]
-        if o["k"] == "dma":
-            fin = s + LDT.get(o["n"], 2.5)
-        free[e] = end[i]
-        for b in o["b"]:
-            bank.setdefault(b, {})[e] = end[i]
-        order.append(i)
-        done += 1
-        for j in succ[i]:
-            est[j] = max(est[j], fin + (WAKE if ops[j]["e"] != e else 0.06))
-            left[j] -= 1
-            if not left[j]:
-                ready.setdefault(ops[j]["e"], []).append(j)
-        end[i] = fin
-    return order, start, end
+GATHERS = ("h", "o", "c", "ch", "xg")
 
 
-def plan(ops):
-    n = len(ops)
-    pred = [o["d"] for o in ops]
-    succ = [[] for _ in ops]
-    for i in range(n):
-        for j in pred[i]:
-            succ[j].append(i)
-    path = [0.0] * n
-    for i in range(n - 1, -1, -1):
-        path[i] = ops[i]["c"] + max([path[j] + WAKE for j in succ[i]], default=0.0)
-    best = None
-    seed = [SEED]
-
-    def rnd():
-        seed[0] = (seed[0] * 1103515245 + 12345) % 2147483648
-        return seed[0] / 1073741824.0 - 1.0
-
-    for lead in LEADS:
-        pri = [p + (lead if o["t"] >= 0 and o["blk"] == 0 else 0.0) for p, o in zip(path, ops)]
-        for _ in range(PASSES):
-            order, start, end = schedule(ops, pri, pred, succ)
-            if best is None or max(end) < max(best[2]):
-                best = (order, start, end)
-            back = schedule(ops, end, succ, pred)[2]
-            pri = [x + NOISE * rnd() for x in back]
-    return best
+def costs(ops, f, gr, net, send):
+    hold, fin = [], []
+    for o in ops:
+        x = o["c"]
+        if o["k"] == "net":
+            x = net
+        elif o["k"] == "send":
+            x = send
+        elif o["k"] == "c":
+            x = f * (0.06 + (x - 0.06) * gr / GR if o["n"] in GATHERS else x)
+        hold.append(x)
+        fin.append(LDT.get(o["n"], 2.5) if o["k"] == "dma" else x)
+    return hold, fin
 
 
-OPS = build()
+def times(order, eng, pred, banks, hold, fin, wake):
+    m = len(order)
+    start, end, why, soft = [0.0] * m, [0.0] * m, [-1] * m, [False] * m
+    free = {e: (0.0, -1) for e in "VAPGSN"}
+    used = [{} for _ in range(8)]
+    for i in order:
+        e = eng[i]
+        t, w = free[e]
+        sf = True
+        for j, same in pred[i]:
+            u = end[j] + (SAME if same else wake)
+            if u > t:
+                t, w, sf = u, j, False
+        for b in banks[i]:
+            for e2, (u, j) in used[b].items():
+                if e2 != e and u + wake > t:
+                    t, w, sf = u + wake, j, True
+        why[i], soft[i], start[i], end[i] = w, sf, t, t + fin[i]
+        if e != "N":
+            free[e] = (t + hold[i], i)
+        for b in banks[i]:
+            used[b][e] = (end[i], i)
+    i = end.index(max(end))
+    pairs = []
+    while why[i] >= 0:
+        if soft[i]:
+            pairs.append((why[i], i))
+        i = why[i]
+    return start, end, pairs
+
+
+def plan(ops, turn):
+    words = turn.split()
+    place = {w.rstrip("+-"): k + len(words) * ((w[-1] == "+") - (w[-1] == "-")) for k, w in enumerate(words)}
+    seen, want, loaded = {}, [], []
+    for o in ops:
+        k = (o["n"], o["blk"], o["t"], o["k"])
+        seen[k] = seen.get(k, 0) + 1
+        name = "%s%d%s" % (o["n"], o["blk"], " bcdefghijklmnop"[min(seen[k], 16) - 1].strip())
+        want.append(place[name] + len(words) * o["t"] if name in place and o["k"] != "net" and o["t"] >= 0 else None)
+        loaded.append(o["k"] == "dma" or any(loaded[j] for j in o["d"]))
+    need = [w if w is not None else 1e5 for w in want]
+    for i in range(len(ops) - 1, -1, -1):
+        for j in ops[i]["d"]:
+            need[j] = min(need[j], need[i])
+    key = []
+    for i, o in enumerate(ops):
+        k = want[i]
+        if k is None:
+            k = need[i] - 0.5 if o["t"] < 0 and loaded[i] and o["k"] != "dma" else need[i] * (o["k"] != "dma") - 1e6
+        key.append(max([k] + [key[j] + 1e-6 for j in o["d"]]))
+    return sorted(range(len(ops)), key=lambda i: key[i])
+
+
+OPS = build(CFG)
 depend(OPS)
-ORDER, START, END = plan(OPS)
+ORDER = plan(OPS, TURN)
+PLACE_OF = {i: k for k, i in enumerate(ORDER)}
 
 SCRATCH = {k: ("sbuf", [128, _size[k]], DTY[k][0]) for k in DTY}
 SCRATCH.update({"ps%d" % k: ("psum", [128, 512], "float32") for k in range(8)})
@@ -527,12 +590,12 @@ def rank_program(g, core, T, topo):
             sig[i] = (o["s"], width)
             snap[i] = {}
             continue
-        deps = {j for j in o["d"] if OPS[j]["k"] != "send"}
+        deps = {j for j in o["d"] if OPS[j]["k"] != "send" and e + OPS[j]["e"] != "PP"}
         for b in o["b"]:
             for e2, j in lastb.get(b, {}).items():
                 if e2 != e:
                     deps.add(j)
-        for j in sorted(deps, key=lambda j: -START[j]):
+        for j in sorted(deps, key=lambda j: -PLACE_OF[j]):
             need(e, j)
         if o["k"] == "send":
             _s, src, land, sem = o["f"]

@@ -17,23 +17,28 @@ GR = 1.56
 NETT = 4.5
 SAME = 0.06
 TURN = """
-Hc0 h0 once1+ twice1+ Rt1+ Oc0 p11+ HcPS0 lin0 p21+ G1+ y1+ I1+ B21+ P0 rz1+ H11+ T0 pU1+ TU1+ h0b C0 H21+ U1+ C160 nO1+ c0 nH1+ h0c ro1+
-zx0 rawh0 c0b sideh0 st0 voteh0 fixh0 maxh0 o0b rawc0 sidec0 fixc0 dh0 Cc0 maxc0 zs1 o0 zx1 dc0 kt1+ voteh0b Hc1 K1+ Oc1 dhS0 sideo0 lin1
-h1b fixo0 rawo0 x0 maxo0 pen0 HcPS1 P1 do0 h1 T1 m0 mw0 zPS1 want0 At0 cntw0 C1 cap0 C161 DC0 am0 DO0 sideh1 c1 rec0 voteh1 fixh1 sel0
-sel20 rawh1 ch160 maxh1 ch0 voteh1b ch0b dh1 splt0 c1b Cc1 vote0 stK0 st1 mx0 vote0b stK1 mx0b g20 sv0 sidec1 o1 Mh0 fixc1 splt0b uraw0
-spl0 ulist0 maxc1 par0 rawc1 ui0 ua0 A0 dc1 fl0 sideo1 fu0 so0 dhS1 p20 o1b ryt0 x1 ayt0 fixo1 zd0 maxo1 u0 pen1 low0 B20 sideo1b ar0 ul0
-fixo1b rawo1 m1 z0 maxo1b l160 once0 twice0 Rt0 mw1 do1 xg0 p10 G0 y0 I0 pU0 rz0 H10 want1 TU0 cntw1 rec1 cap1 U0 H20 am1 nO0 sel1 nH0
-sel21 At1 ro0 ch161 DO1 ch1 ch1b ct0 splt1 DC1 g21 ch1c mx1b vote1 xf0 mx1 vote1b mx1c scat0 ulist1 sv1 yes0 splt1b ui1 ryt1 ua1 ct1
-uraw1 ul1 yes1 ayt1 fu1 l161 zPS0- spl1 xg1 Mh1 A1 par1 zs0- u1 xf1 fl1 scat1 ar1 zd1 z1 so1 low1
+h0 p11+ rq1+ so1+ P0 p21+ G1+ y1+ I1+ T0 zx0p B21+ A1+ C0 H11+ zx0g pU1+ h0b C160 H21+ TU1+ kt1+ rz1+ c0 U1+ nH1+ nO1+ h0c zx0i ro1+ c0b
+c0c rawh0 zx0n sideh0 o0 zx1p rawc0 sidec0 fixh0 zx1c fixc0 maxh0 zx1n zx1 o0b maxc0 zx1o dh0 zx1f voteh0 zx1k st0 Hc1 dc0 dhS0 zx1m
+sideo0 h1 fixo0 zPS1 lin1 zx1i HcPS1 x0 maxo0 zx1g pen0 rawo0 zx1h K1+ m0 zx1l h1b P1 do0 mw0 zx1d T1 At0 zx1b want0 cntw0 C1 zx1j C161
+cap0 rec0 zx1e st1 am0 Cc0 sel0 c1 sideh1 sel20 DC0 rawh1 ch160 stK1 ch0b voteh0b splt0 ch0 voteh1 voteh1b mx0b Cc1 fixh1 c1b maxh1
+vote0 vote0b stK0 mx0 sv0 sidec1 o1 splt0b ulist0 spl0 fixc1 dh1 A0 maxc1 zd0 par0 rawc1 z0 sideo1 o1b fl0 rq0 uraw0 fixo1 dc1 so0
+maxo1 ayt0 ryt0 DO0 dhS1 ui0 g20 sideo1b ar0 fixo1b rawo1 x1 low0 maxo1b fu0 pen1 p10 do1 p20 m1 ua0 mw1 once0 twice0 Rt0 u0 ul0 want1
+B20 cntw1 l160 pU0 cap1 H10 rec1 zx0k- TU0 am1 xg0 sel1 U0 zx0f- sel21 H20 At1 zx0- ch161 splt1 nO0 nH0 ch1b DC1 ch1 ct0 ro0 zx0o- xf0
+ch1c mx1 vote1 zx0d- mx1b zx0h- yes0 mx1c vote1b zx0l- scat0 ulist1 zx0b- sv1 G0 y0 I0 zx0c- splt1b ui1 ayt1 ua1 ct1 zx0e- ryt1 ul1 zd1
+zPS0- yes1 uraw1 l161 spl1 DO1 zx0m- xg1 fu1 par1 low1 xf1 Hc0- g21 rz0 ar1 u1 scat1 HcPS0- z1 zx0j- once1 twice1 Rt1 lin0- fl1
 """
+EARLY = ("Hc0", "HcPS0", "lin0", "P0", "T0", "C0", "C160")
+SOON = "want0"
 CFG = {
-    "col": [{"h": "A4A2V2", "o": "A4A4", "c": "A4A4"}, {"h": "A4A4", "o": "A5A3", "c": "A4A4"}],
+    "col": [{"h": "A4A1V3", "o": "A4A4", "c": "A4A2V2"}, {"h": "A4A4", "o": "A5A3", "c": "A4A4"}],
     "cut": [{"h": "V8", "o": "V8", "c": "V8"}, {"h": "V8", "o": "V5V3", "c": "V8"}],
-    "ch": ["A5V3", "V3A3A2"],
-    "side": "V", "zs": "A", "dhS": "A", "mails": 2, "zx": "VV", "xg": "AA", "zmail": False,
+    "sum": [{"h": "P8", "o": "P8", "c": "P8"}, {"h": "P8", "o": "P8", "c": "P8"}],
+    "ch": ["A4V4", "V3A3A2"],
+    "side": ["VVV", "GGV"], "zs": "A", "dhS": "A", "mails": 2, "zx": "GG", "xg": "VV", "zmail": [True, True], "zxa": [0, 0],
+    "pad": False, "quick": [True, True], "stK": "V", "fl": "VV",
 }
 
-DTY = {"aw": ("bfloat16", 2), "af": ("float32", 4), "ai": ("int32", 4), "au": ("uint16", 2), "ah": ("float16", 2)}
+DTY = {"aw": ("bfloat16", 2), "af": ("float32", 4), "ai": ("int32", 4), "au": ("uint16", 2), "ah": ("float16", 2), "a3": ("bfloat16", 2)}
 _size = {k: 0 for k in DTY}
 
 
@@ -53,7 +58,23 @@ def ps(bank, slot, m=n):
 
 
 def ncol(h):
+    if h[-1] == "bills":
+        return (h[2] - h[1]) // 17 * 16
     return (h[2] - h[1] + h[3] - 1) // h[3]
+
+
+def view(T, h):
+    if isinstance(h, str):
+        return T[h][:]
+    if h[0] == "a3":
+        a, b = h[1] // 17, (h[2] + 16) // 17
+        if h[3] == 17:
+            return T["a3"][:, a:a + ncol(h), h[1] % 17]
+        return T["a3"][:, a:b, 1:17] if h[-1] == "bills" else T["a3"][:, a:b, :]
+    p0, p1 = h[4:] or (0, 128)
+    if h[3] == 1:
+        return T[h[0]][p0:p1, h[1]:h[2]]
+    return T[h[0]][p0:p1, h[1]:h[2]:h[3]]
 
 
 def wide(h):
@@ -163,14 +184,14 @@ def build(cfg):
     ONE = new("aw", 128)
     ID, BO, BN, LT, T1, LS, LQ, WB = [new("aw", 128) for _ in range(8)]
     MID = {v: new("aw", 128) for v in (-1, 0.5, -0.5, 1.25, 32, -32, -64, -128, 145, SEG, BIG, 2 * BIG, 0.5 / BIG, -4096,
-                                       -2.0 ** -10, -2.0 ** -17, 2.0 ** -30)}
+                                       -2.0 ** -10, -2.0 ** -17, 2.0 ** -30, -2.0 ** -30)}
     HID = {v: new("ah", 128) for v in (1, -1, 0.5, 32, 2080, 3232, 2.0 ** -12, -2.0 ** -12)}
-    FID = {v: new("af", 128) for v in (1, 0.5, 2.0 ** -12)}
+    FID = {v: new("af", 128) for v in (1, 0.5, 32, 2.0 ** -12)}
     HALF = new("af", 128)
     G1, G2, GM = new("aw", 8), new("aw", 8), new("aw", 8)
     D, WD = new("aw", 144), new("aw", 144)
     ZERO, CONST = new("aw", n), new("aw", 5 * n)
-    MASK = new("aw", 16 * n)
+    MASK = new("aw", 16 * n if "V" in cfg["zx"] else 16 * max(q1 - q0 for x in cfg["ch"] for _e, q0, q1 in pieces(x)))
     NEG, HI = MID[-1], HID[1]
 
     vset(ONE, 1.0)
@@ -204,7 +225,7 @@ def build(cfg):
     for k, v in enumerate((129.0 * 4096, 65536.0 - 2.0 ** 23, 2048.0 - BIG, 113.0, 103.0)):
         vset(part(k), v)
     vset(MASK, 1.0)
-    vset(sub(MASK, 0, 16 * n, 16), 0.0)
+    vset(sub(MASK, 0, ncol(MASK), 16), 0.0)
     B1, B2, BASE = new("ai", n // 16), new("ai", n // 16), new("ai", n // 16)
     iota(B1, [[0, n // 16]], 0, 16)
     iota(B2, [[256, n // 16]], 0, 0)
@@ -214,26 +235,35 @@ def build(cfg):
     I1, I2, PLACE = new("ai", n), new("ai", n), new("ah", n)
     F1, F2 = new("af", n), new("af", n)
     iota(J, [[0, 1]], 0, 1)
-    iota(I1, [[16, n]], n - 1024, 0)
-    iota(I2, [[15, n]], n, 0)
     vts(J, J, 15, None, OP.bitwise_and)
     vcopy(JF, J)
-    vts(J0, JF, 0.0, None, OP.is_equal)
-    vts(F1, I1, JF, None, OP.add)
-    vts(F2, I2, J0, None, OP.mult)
-    vtt(PLACE, F1, F2, OP.subtract)
+    if cfg["pad"]:
+        iota(I1, [[17, n]], 1 - 1024, 0)
+        vts(PLACE, I1, JF, None, OP.add)
+    else:
+        iota(I1, [[16, n]], n - 1024, 0)
+        iota(I2, [[15, n]], n, 0)
+        vts(J0, JF, 0.0, None, OP.is_equal)
+        vts(F1, I1, JF, None, OP.add)
+        vts(F2, I2, J0, None, OP.mult)
+        vtt(PLACE, F1, F2, OP.subtract)
 
     big = []
     ZS = new("aw", 16 * n)
-    vset(ZS, 0.0)
+    if "V" in cfg["zx"]:
+        vset(ZS, 0.0)
     for b in range(NB):
-        d = {k: new("aw", 16 * n) for k in ("mh", "mo", "mc", "ch", "mx", "zx")}
+        d = {k: new("aw", SEG) for k in ("mh", "mo", "mc", "ch", "mx", "zx")}
         d["zs"] = ZS
-        d["win"] = new("aw", 3 * SEG)
+        d["win"] = new("a3" if cfg["pad"] else "aw", 3 * SEG)
+        if cfg["pad"]:
+            vset(sub(d["win"], 0, 3 * SEG, 17), 255.0)
+            vset(sub(d["zx"], 0, SEG, 17), 0.0)
         d.update({k: new("aw", n) for k in ("st", "rec", "want", "cnt", "am", "sv", "spl", "low", "x", "fl", "so", "fu", "g1", "g2")})
         d["ar"], d["yes"], d["p1"] = new("aw", 2 * n), new("aw", 8), new("af", 2 * n)
-        d.update({k: new("ah", n) for k in ("Hc", "Oc", "Cc", "stK")})
-        d.update({k: new("af", n) for k in ("dhS", "m", "mw", "xg", "P", "pU", "p2", "A")})
+        d.update({k: new("ah", n) for k in ("Cc", "stK")})
+        d["ABc"] = new("ah", 2 * n)
+        d.update({k: new("af", n) for k in ("dhS", "m", "mw", "xg", "P", "pU", "p2", "A", "stF")})
         d.update({k: new("ai", n) for k in ("T", "C", "TU", "xf")})
         d.update({k: new("ai", n // 16) for k in ("ui", "ua", "ul")})
         d["C16"], d["ch16"], d["l16"] = new("au", n), new("au", n), new("au", n // 16)
@@ -244,10 +274,26 @@ def build(cfg):
 
     mail = []
     for b in range(NB):
-        A16, B16 = new("au", n), new("au", n)
+        AB = new("au", 2 * n)
+        A16, B16 = sub(AB, 0, n), sub(AB, n, 2 * n)
         vcopy(A16, sub(bain, n * b, n * b + n))
         vcopy(B16, sub(bbin, n * b, n * b + n))
-        mail.append((A16, B16, sub(zin, n * b, n * b + n), ONE, None, ONE))
+        mail.append((A16, B16, sub(zin, n * b, n * b + n), ONE, None, ONE, AB))
+
+    def after(k, d, raw, vs, dh, dc, dp, R):
+        if k == "h":
+            pe(vs, [(NEG, raw[j]) for j in range(8)], "voteh", stop=False)
+            pe(vs, [(NEG, raw[j]) for j in range(8, 16)], "voteh", first=False, stop=False)
+            copy(cfg["dhS"], d["dhS"], dh, "dhS")
+        if k == "c":
+            if cfg["quick"][cur[1]]:
+                vtt(d["x"], d["dhS"], dc, OP.is_le, "x")
+            vtt(d["m"], d["dhS"], dc, OP.min, "m")
+            if cfg["quick"][cur[1]]:
+                pe(dp, [(R, MID[2.0 ** -30]), (d["st"], ID), (ID, d["x"])], "pen")
+                vtt(d["mw"], d["m"], dp, OP.max, "mw")
+            else:
+                pe(dp, [(FID[1], d["dhS"]), (R, MID[-2.0 ** -30]), (d["st"], NEG)], "pen", stop=False)
 
     for t in range(NREAD):
         last = t == NREAD - 1
@@ -258,9 +304,10 @@ def build(cfg):
             Bd, Bv, Bx, By = b, 2 + b, 4 + b, 6 + b
             H16, O16, z, R = mail[b][t & 1], mail[b][1 - (t & 1)], mail[b][2], mail[b][5]
             hp, lin, zp, sel = [ps(Bx, k) for k in range(4)]
-            vts(d["Hc"], H16, -2048.0, None, OP.add, name="Hc")
-            vts(d["Oc"], O16, -2048.0, None, OP.add, name="Oc")
-            pe(zp, [(ID, z)], "zPS")
+            d["Hc"], d["Oc"] = [sub(d["ABc"], k * n, k * n + n) for k in (t & 1, 1 - (t & 1))]
+            vts(d["ABc"], mail[b][6], -2048.0, None, OP.add, name="Hc")
+            if not cfg["pad"]:
+                pe(zp, [(ID, z)], "zPS")
             pe(hp, [(HI, d["Hc"])], "HcPS")
             pe(lin, [(HID[2080], d["Hc"]), (HID[3232], d["Oc"])], "lin")
             vtt(d["P"], d["Oc"], hp, OP.mult, "P")
@@ -271,7 +318,7 @@ def build(cfg):
             vtt(d["st"], d["Oc"], hp, OP.is_equal, "st")
             if cfg["zx"][b] == "G":
                 for j in range(16):
-                    copy("G", sub(d["zx"], j, 16 * n, 16), z, "zx")
+                    copy("A" if j < cfg["zxa"][b] else "G", sub(d["zx"], j + 1, SEG, 17) if cfg["pad"] else sub(d["zx"], j, 16 * n, 16), z, "zx")
             else:
                 copy(cfg["zs"], sub(d["zs"], 0, 16 * n, 16), z, "zs")
                 scan(d["zx"], MASK, d["zs"], OP.mult, OP.add, "zx")
@@ -279,31 +326,43 @@ def build(cfg):
             vs, dp = ps(Bv, 0), ps(By, 1)
             for k, lst, dist in (("h", H16, dh), ("c", d["C16"], dc), ("o", O16, do)):
                 at = SEG * "hoc".index(k)
+                if cfg["pad"]:
+                    col, res = sub(d["win"], at, at + SEG), d["m" + k]
+                    for e, q0, q1 in pieces(cfg["col"][b][k]):
+                        gath(e, sub(col, 17 * q0, 17 * q1) + ("bills",), X, sub(lst, q0, q1), name=k)
+                    for _e, q0, q1 in pieces(cfg["cut"][b][k]):
+                        scan(sub(res, 17 * q0, 17 * q1), sub(d["zx"], 17 * q0, 17 * q1), sub(col, 17 * q0, 17 * q1), OP.min, OP.max, "max" + k)
+                    raw = [sub(col, j + 1, SEG, 17) for j in range(16)]
+                    opening = (d["st"], MID[0.5 / BIG], dist) if k == "o" else (ID, ZERO, dist)
+                    pe(None, [opening] + [(raw[j], GM, sub(dist, j, n, 16)) for j in range(16)], "raw" + k, stop=False)
+                    pe(None, [(sub(res, j + 1, SEG, 17), G2, sub(dist, j, n, 16)) for j in range(16)], "d" + k, first=False)
+                    after(k, d, raw, vs, dh, dc, dp, R)
+                    continue
                 side, col, res = sub(d["win"], at, at + n), sub(d["win"], at + n, at + SEG), d["m" + k]
                 for e, q0, q1 in pieces(cfg["col"][b][k]):
                     gath(e, sub(col, 16 * q0, 16 * q1), X, sub(lst, q0, q1), name=k)
                 for _e, q0, q1 in pieces(cfg["cut"][b][k]):
                     head = sub(col, 16 * q0, 16 * q1, 16)
-                    copy(cfg["side"], sub(side, q0, q1), head, "side" + k)
+                    copy(cfg["side"][b]["hco".index(k)], sub(side, q0, q1), head, "side" + k)
                     vtt(head, head, sub(zp, q0, q1), OP.max, "fix" + k)
                     scan(sub(res, 16 * q0, 16 * q1), sub(d["zx"], 16 * q0, 16 * q1), sub(col, 16 * q0, 16 * q1), OP.min, OP.max, "max" + k)
                 raw = [side] + [sub(col, j, 16 * n, 16) for j in range(1, 16)]
                 opening = (d["st"], MID[0.5 / BIG], dist) if k == "o" else (ID, ZERO, dist)
-                pe(None, [opening] + [(raw[j], GM, sub(dist, j, n, 16)) for j in range(1, 16)], "raw" + k, stop=False)
-                pe(None, [(side, GM, sub(dist, 0, n, 16))] + [(sub(res, j, 16 * n, 16), G2, sub(dist, j, n, 16)) for j in range(16)], "d" + k, first=False)
-                if k == "h":
-                    pe(vs, [(NEG, raw[j]) for j in range(8)], "voteh", stop=False)
-                    pe(vs, [(NEG, raw[j]) for j in range(8, 16)], "voteh", first=False, stop=False)
-                    copy(cfg["dhS"], d["dhS"], dh, "dhS")
-
-                if k == "c":
-                    vtt(d["x"], d["dhS"], dc, OP.is_le, "x")
-                    vtt(d["m"], d["dhS"], dc, OP.min, "m")
-                    pe(dp, [(R, MID[2.0 ** -30]), (d["st"], ID), (ID, d["x"])], "pen")
-                    vtt(d["mw"], d["m"], dp, OP.max, "mw")
+                for _e, q0, q1 in pieces(cfg["sum"][b][k]):
+                    rows = [sub(dist, j, n, 16) + (q0, q1) for j in range(16)]
+                    pe(None, [opening] * (q0 == 0) + [(sub(col, 16 * q0 + j, 16 * q1, 16), GM, rows[j]) for j in range(1, 16)], "raw" + k,
+                       first=q0 == 0, stop=False)
+                    pe(None, [(sub(side, q0, q1), GM, rows[0])] + [(sub(res, 16 * q0 + j, 16 * q1, 16), G2, rows[j]) for j in range(16)],
+                       "d" + k, first=False, stop=q1 == n)
+                after(k, d, raw, vs, dh, dc, dp, R)
             cap = ps(By, 0)
-            vtt(d["want"], d["mw"], do, OP.is_lt, "want")
-            vtt(d["rec"], d["m"], do, OP.is_ge, "rec")
+            if cfg["quick"][b]:
+                vtt(d["want"], d["mw"], do, OP.is_lt, "want")
+                vtt(d["rec"], d["m"], do, OP.is_ge, "rec")
+            else:
+                vtt(d["rec"], d["m"], do, OP.is_ge, "rec")
+                pe(dp, [(NEG, d["rec"])], "penr", first=False)
+                vtt(d["want"], d["m"], dp, OP.is_lt, "want")
             scan(d["cnt"], sub(MASK, 0, n), d["want"], OP.mult, OP.add, "cntw")
             pe(sel, [(HI, PLACE), (d["rec"], MID[SEG])], "sel", stop=False)
             pe(cap, [(d["want"], MID[-64]), (d["cnt"], ID)], "cap")
@@ -371,10 +430,15 @@ def build(cfg):
             pe(None, [(BO, d["sv"], ps(By, 0)), (MID[32], d["am"], ps(By, 0))], "ayt")
             pe(None, [(BO, d["sv"], ps(By, 1)), (d["rec"], MID[32], ps(By, 1))], "ryt")
             act(d["ar"], ps(By, 0, 2 * n), AF.Sign, bias=-31.0, name="ar")
-            if t > 0:
+            more = []
+            if t > 0 and cfg["stK"] == "V":
                 vts(d["stK"], st, KC[t - 1], None, OP.mult, name="stK")
-            pe(None, [(ID, sub(CONST, 0, 2 * n), ps(Bd, 0, 2 * n)), (HID[32], Oc, Lt)]
-               + ([(HID[32], d["stK"], Lt)] if t > 0 else []), "g2", stop=False)
+                more = [(HID[32], d["stK"], Lt)]
+            elif t > 0:
+                add("A", AO + CY * n, [st, KC[t - 1]], [d["stF"]],
+                    lambda q, V, d=d, k=KC[t - 1]: q.activation(V(d["stF"]), V(d["st"]), AF.Copy, 0.0, V(k)), "stK")
+                more = [(FID[32], d["stF"], Lt)]
+            pe(None, [(ID, sub(CONST, 0, 2 * n), ps(Bd, 0, 2 * n)), (HID[32], Oc, Lt)] + more, "g2", stop=False)
             pe(ur, [(WB, M)], "uraw")
             act(d["fu"], ur, AF.Copy, scale=1.0 / 4096, bias=128.5 + 1.0 / 8192, name="fu")
             pe(Bt, [(MID[-4096], d["fu"]), (WB, M), (HID[-2.0 ** -12], Oc), (HID[2.0 ** -12], Hc)], "u", first=False, stop=False)
@@ -394,7 +458,7 @@ def build(cfg):
                 pe(Rt, [(MID[145], part(3)), (MID[2 * BIG], ay)], "Rt")
                 vtt(out["G"], R, Rt, OP.mult, "G")
                 zl, la = new("aw", 4 * n), new("au", 2 * n)
-                if cfg["zmail"]:
+                if cfg["zmail"][b]:
                     mailto(out["z"], sub(zl, 0, n), "rq", t, b)
                     mailto(sub(out["ZIG"], n, 4 * n), sub(zl, n, 4 * n), "rz", t, b)
                 else:
@@ -407,7 +471,7 @@ def build(cfg):
                 pe(Rt, [(ID, d["g1"]), (ID, d["g2"]), (MID[0.5], ay)], "Rt")
                 act(out["G"], Rt, AF.Copy, bias=0.5, name="G")
             vtt(d["A"], spl, At, OP.max, "A")
-            act(d["fl"], par, AF.Copy, name="fl")
+            copy(cfg["fl"][b], d["fl"], par, "fl")
             vtt(d["so"], d["fl"], par, OP.is_equal, "so")
             vtt(d["p2"], d["so"], DC, OP.mult, "p2")
             pe(Bt, [(FID[2.0 ** -12], d["p2"])], "B2", first=False)
@@ -426,7 +490,7 @@ def build(cfg):
                     mailto(oo, la_o, "ro", t, b)
                 else:
                     mailto(out["AB"], la, "ro", t, b)
-                nxt.append((sub(la, 0, n), sub(la, n, 2 * n)) + tuple(sub(zl, k * n, k * n + n) for k in range(4)))
+                nxt.append((sub(la, 0, n), sub(la, n, 2 * n)) + tuple(sub(zl, k * n, k * n + n) for k in range(4)) + (la,))
             else:
                 for k, nme in (("G", "yg"), ("I", "yi"), ("A", "ya"), ("B", "yb")):
                     add("S", 0.1, [out[k]], [], lambda q, V, nme=nme, h=out[k], a=n * b: q.dma_start(V(nme)[:, a:a + n], V(h)), "st" + nme, "dma", "st%s%d" % (nme, b))
@@ -525,6 +589,8 @@ def plan(ops, turn):
         seen[k] = seen.get(k, 0) + 1
         name = "%s%d%s" % (o["n"], o["blk"], " bcdefghijklmnop"[min(seen[k], 16) - 1].strip())
         want.append(place[name] + len(words) * o["t"] if name in place and o["k"] != "net" and o["t"] >= 0 else None)
+        if o["t"] == 0 and name in EARLY:
+            want[-1] -= 5e5
         loaded.append(o["k"] == "dma" or any(loaded[j] for j in o["d"]))
     need = [w if w is not None else 1e5 for w in want]
     for i in range(len(ops) - 1, -1, -1):
@@ -534,7 +600,12 @@ def plan(ops, turn):
     for i, o in enumerate(ops):
         k = want[i]
         if k is None:
-            k = need[i] - 0.5 if o["t"] < 0 and loaded[i] and o["k"] != "dma" else need[i] * (o["k"] != "dma") - 1e6
+            if o["t"] >= 0 or o["k"] == "dma":
+                k = -2e6
+            elif loaded[i]:
+                k = need[i] - 0.5
+            else:
+                k = need[i] - (1e6 if need[i] <= place[SOON] else 1e5)
         key.append(max([k] + [key[j] + 1e-6 for j in o["d"]]))
     return sorted(range(len(ops)), key=lambda i: key[i])
 
@@ -544,7 +615,7 @@ depend(OPS)
 ORDER = plan(OPS, TURN)
 PLACE_OF = {i: k for k, i in enumerate(ORDER)}
 
-SCRATCH = {k: ("sbuf", [128, _size[k]], DTY[k][0]) for k in DTY}
+SCRATCH = {k: ("sbuf", [128, _size[k] // 17, 17] if k == "a3" else [128, _size[k]], DTY[k][0]) for k in DTY if _size[k]}
 SCRATCH.update({"ps%d" % k: ("psum", [128, 512], "float32") for k in range(8)})
 SEMAPHORES = ["cV", "cA", "cP", "cG", "sent"] + sorted({o["s"] for o in OPS if o["s"]})
 
@@ -560,11 +631,7 @@ def rank_program(g, core, T, topo):
     queue = {"V": g.vector, "A": g.scalar, "P": g.tensor, "G": g, "S": g.sync}
 
     def V(h):
-        if isinstance(h, str):
-            return T[h][:]
-        if h[3] == 1:
-            return T[h[0]][:, h[1]:h[2]]
-        return T[h[0]][:, h[1]:h[2]:h[3]]
+        return view(T, h)
 
     count = {e: 0 for e in "VAPG"}
     know = {e: {} for e in queue}

import math
from concourse.bass import DstId, RemoteDMATransfer
from concourse.mybir import AluOpType, AxisListType, ActivationFunctionType

OP = AluOpType
AF = ActivationFunctionType
W, NP, NREAD = 4096, 256, 6
NB, n = 2, 128
SEG = 17 * n
SLOT = 128
BIG = 8192.0
CY = 0.00083
PECY = 0.00042
PEO = 0.008
VO, AO = 0.045, 0.06
GR = 1.56
NETT = 4.5
SAME = 0.06
TURN = """
h0 p11+ rq1+ so1+ P0 p21+ G1+ y1+ I1+ T0 zx0p B21+ A1+ C0 H11+ zx0g pU1+ h0b C160 H21+ TU1+ kt1+ rz1+ c0 U1+ nH1+ nO1+ h0c zx0i ro1+ c0b
c0c rawh0 zx0n sideh0 o0 zx1p rawc0 sidec0 fixh0 zx1c fixc0 maxh0 zx1n zx1 o0b maxc0 zx1o dh0 zx1f voteh0 zx1k st0 Hc1 dc0 dhS0 zx1m
sideo0 h1 fixo0 zPS1 lin1 zx1i HcPS1 x0 maxo0 zx1g pen0 rawo0 zx1h K1+ m0 zx1l h1b P1 do0 mw0 zx1d T1 At0 zx1b want0 cntw0 C1 zx1j C161
cap0 rec0 zx1e st1 am0 Cc0 sel0 c1 sideh1 sel20 DC0 rawh1 ch160 stK1 ch0b voteh0b splt0 ch0 voteh1 voteh1b mx0b Cc1 fixh1 c1b maxh1
vote0 vote0b stK0 mx0 sv0 sidec1 o1 splt0b ulist0 spl0 fixc1 dh1 A0 maxc1 zd0 par0 rawc1 z0 sideo1 o1b fl0 rq0 uraw0 fixo1 dc1 so0
maxo1 ayt0 ryt0 DO0 dhS1 ui0 g20 sideo1b ar0 fixo1b rawo1 x1 low0 maxo1b fu0 pen1 p10 do1 p20 m1 ua0 mw1 once0 twice0 Rt0 u0 ul0 want1
B20 cntw1 l160 pU0 cap1 H10 rec1 zx0k- TU0 am1 xg0 sel1 U0 zx0f- sel21 H20 At1 zx0- ch161 splt1 nO0 nH0 ch1b DC1 ch1 ct0 ro0 zx0o- xf0
ch1c mx1 vote1 zx0d- mx1b zx0h- yes0 mx1c vote1b zx0l- scat0 ulist1 zx0b- sv1 G0 y0 I0 zx0c- splt1b ui1 ayt1 ua1 ct1 zx0e- ryt1 ul1 zd1
zPS0- yes1 uraw1 l161 spl1 DO1 zx0m- xg1 fu1 par1 low1 xf1 Hc0- g21 rz0 ar1 u1 scat1 HcPS0- z1 zx0j- once1 twice1 Rt1 lin0- fl1
"""
EARLY = ("Hc0", "HcPS0", "lin0", "P0", "T0", "C0", "C160")
SOON = "want0"
CFG = {
    "col": [{"h": "A4A1V3", "o": "A4A4", "c": "A4A2V2"}, {"h": "A4A4", "o": "A5A3", "c": "A4A4"}],
    "cut": [{"h": "V8", "o": "V8", "c": "V8"}, {"h": "V8", "o": "V5V3", "c": "V8"}],
    "sum": [{"h": "P8", "o": "P8", "c": "P8"}, {"h": "P8", "o": "P8", "c": "P8"}],
    "ch": ["A4V4", "V3A3A2"],
    "side": ["VVV", "GGV"], "zs": "A", "dhS": "A", "mails": 2, "zx": "GG", "xg": "VV", "zmail": [True, True], "zxa": [0, 0],
    "pad": False, "quick": [True, True], "stK": "V", "fl": "VV",
}

DTY = {"aw": ("bfloat16", 2), "af": ("float32", 4), "ai": ("int32", 4), "au": ("uint16", 2), "ah": ("float16", 2), "a3": ("bfloat16", 2)}
_size = {k: 0 for k in DTY}


def new(ar, m):
    a = _size[ar]
    step = 32 // DTY[ar][1]
    _size[ar] = a + (m + step - 1) // step * step
    return (ar, a, a + m, 1)


def sub(h, a, b, s=1):
    return (h[0], h[1] + a, h[1] + b, s)


def ps(bank, slot, m=n):
    return ("ps%d" % bank, slot * SLOT, slot * SLOT + m, 1)


def ncol(h):
    if h[-1] == "bills":
        return (h[2] - h[1]) // 17 * 16
    return (h[2] - h[1] + h[3] - 1) // h[3]


def view(T, h):
    if isinstance(h, str):
        return T[h][:]
    if h[0] == "a3":
        a, b = h[1] // 17, (h[2] + 16) // 17
        if h[3] == 17:
            return T["a3"][:, a:a + ncol(h), h[1] % 17]
        return T["a3"][:, a:b, 1:17] if h[-1] == "bills" else T["a3"][:, a:b, :]
    p0, p1 = h[4:] or (0, 128)
    if h[3] == 1:
        return T[h[0]][p0:p1, h[1]:h[2]]
    return T[h[0]][p0:p1, h[1]:h[2]:h[3]]


def wide(h):
    return 4 if h[0] not in DTY else DTY[h[0]][1]


def pieces(text):
    out, at = [], 0
    for e, k in zip(text[::2], text[1::2]):
        out.append((e, at, at + int(k) * n // 8))
        at = out[-1][2]
    return out


def build(cfg):
    ops = []
    cur = [-1, 0]
    for k in _size:
        _size[k] = 0

    def add(eng, cost, reads, writes, emit, name="", kind="c", sem=None, extra=(), grp=None):
        ops.append({"e": eng, "c": cost, "r": reads, "w": writes, "f": emit, "n": name, "k": kind, "s": sem, "x": list(extra),
                    "t": cur[0], "blk": cur[1], "g": grp})
        return len(ops) - 1

    def vts(o, i, s1, s2, op0, op1=None, name="ts"):
        fast = wide(o) == 2 and wide(i) == 2
        rd = [i] + [s for s in (s1, s2) if isinstance(s, tuple)]

        def f(q, V):
            a = V(s1) if isinstance(s1, tuple) else s1
            if op1 is None:
                return q.tensor_scalar(V(o), V(i), a, None, op0)
            b = V(s2) if isinstance(s2, tuple) else s2
            return q.tensor_scalar(V(o), V(i), a, b, op0, op1)
        return add("V", VO + CY * max(64, ncol(o) * (0.5 if fast else 1)), rd, [o], f, name)

    def vtt(o, a, b, op, name="tt"):
        both = a[0] in DTY and b[0] in DTY
        return add("V", VO + CY * max(64, ncol(o) * (2 if both else 1)), [a, b], [o], lambda q, V: q.tensor_tensor(V(o), V(a), V(b), op), name)

    def vcopy(o, i, name="cp"):
        fast = wide(o) == 2 and wide(i) == 2
        return add("V", VO + CY * max(64, ncol(o) * (0.5 if fast else 1)), [i], [o], lambda q, V: q.tensor_copy(V(o), V(i)), name)

    def vset(o, v):
        return add("V", VO + CY * max(64, ncol(o) * (0.5 if wide(o) == 2 else 1)), [], [o], lambda q, V: q.memset(V(o), v), "set")

    def scan(o, a, b, op0, op1, name):
        return add("V", VO + CY * max(64, ncol(o) / 2), [a, b], [o], lambda q, V: q.tensor_tensor_scan(V(o), V(a), V(b), 0.0, op0, op1), name)

    def act(o, i, fn, scale=1.0, bias=0.0, acc=None, name="act"):
        def f(q, V):
            if acc is None:
                return q.activation(V(o), V(i), fn, bias, scale)
            return q.activation(V(o), V(i), fn, bias, scale, accum_out=V(acc))
        return add("A", AO + CY * max(64, ncol(o)), [i], [o] + ([acc] if acc else []), f, name)

    def asel(o, i, pat, cmp, base, cm, name="asel"):
        return add("G", 0.17 + 2 * CY * ncol(o), [i], [o], lambda q, V: q.affine_select(V(o), V(i), pat, cmp, 0.0, base, cm), name)

    def iota(o, pat, base, cm):
        return add("G", 0.13 + 2 * CY * ncol(o), [], [o], lambda q, V: q.iota(V(o), pat, base, cm), "iota")

    def copy(eng, o, i, name):
        if eng == "A":
            return act(o, i, AF.Copy, name=name)
        if eng == "G":
            return asel(o, i, [[0, ncol(o)]], OP.is_ge, 0, 0, name)
        return vcopy(o, i, name)

    def gath(eng, o, win, off, other=None, op=None, name="gather"):
        m = ncol(o)
        if eng == "A":
            return add("A", 0.065 + CY * GR * m, [win, off], [o],
                       lambda q, V: q.activation(V(o), V(win).indirect(V(off)), AF.Copy), name)
        if other is None:
            return add("V", 0.05 + CY * GR * m, [win, off], [o],
                       lambda q, V: q.tensor_copy(V(o), V(win).indirect(V(off))), name)
        return add("V", 0.05 + CY * GR * m, [win, off, other], [o],
                   lambda q, V: q.tensor_tensor(V(o), V(win).indirect(V(off)), V(other), op), name)

    def pe(o, terms, name="pe", first=True, stop=True):
        terms = [(x[0], x[1], x[2] if len(x) > 2 else o) for x in terms]
        c = 0.03
        for l, r, _o in terms:
            c += PEO + PECY * max(min(64, ncol(l)), ncol(r)) * (4 if l[0] == "af" else 1)

        def f(q, V):
            last = None
            for k, (l, r, out) in enumerate(terms):
                last = q.matmul(V(out), V(l), V(r), first and k == 0, stop and k == len(terms) - 1)
            return last
        return add("P", c, [x for t in terms for x in t[:2]], sorted({t[2] for t in terms}), f, name, grp=(terms[0][2][0], first, stop))

    def mailto(src, land, nm, t, b):
        sem = "%s%d_%d" % (nm, t, b)
        k = add("G", 1.0, [src], [], ("send", src, land, sem), nm, "send")
        add("N", NETT, [], [land], None, nm, "net", sem, (k,))

    X = new("aw", W)
    zin, win_ = new("aw", NP), new("aw", 1)
    bain, bbin = new("ai", NP), new("ai", NP)
    for nm, h in (("ba", bain), ("bb", bbin), ("zp", zin), ("wl", win_), ("xt", X)):
        add("S", 0.1, [], [h], lambda q, V, nm=nm, h=h: q.dma_start(V(h), V(nm)), "ld" + nm, "dma", "ld" + nm)

    ONE = new("aw", 128)
    ID, BO, BN, LT, T1, LS, LQ, WB = [new("aw", 128) for _ in range(8)]
    MID = {v: new("aw", 128) for v in (-1, 0.5, -0.5, 1.25, 32, -32, -64, -128, 145, SEG, BIG, 2 * BIG, 0.5 / BIG, -4096,
                                       -2.0 ** -10, -2.0 ** -17, 2.0 ** -30, -2.0 ** -30)}
    HID = {v: new("ah", 128) for v in (1, -1, 0.5, 32, 2080, 3232, 2.0 ** -12, -2.0 ** -12)}
    FID = {v: new("af", 128) for v in (1, 0.5, 32, 2.0 ** -12)}
    HALF = new("af", 128)
    G1, G2, GM = new("aw", 8), new("aw", 8), new("aw", 8)
    D, WD = new("aw", 144), new("aw", 144)
    ZERO, CONST = new("aw", n), new("aw", 5 * n)
    MASK = new("aw", 16 * n if "V" in cfg["zx"] else 16 * max(q1 - q0 for x in cfg["ch"] for _e, q0, q1 in pieces(x)))
    NEG, HI = MID[-1], HID[1]

    vset(ONE, 1.0)
    asel(ID, ONE, [[-1, 128]], OP.is_equal, 0, 1)
    asel(T1, ONE, [[-16, 8], [0, 16]], OP.is_ge, 0, 1)
    asel(BO, T1, [[16, 8], [0, 16]], OP.is_ge, 15, -1)
    asel(LT, BO, [[1, 128]], OP.is_gt, 0, -1)
    for v in sorted(HID):
        vts(HID[v], ID, float(v), None, OP.mult)
    for v in sorted(MID):
        act(MID[v], ID, AF.Copy, scale=float(v))
    for v in sorted(FID):
        act(FID[v], ID, AF.Copy, scale=float(v))
    vset(HALF, -0.5)
    act(LS, LT, AF.Copy, scale=2.0 ** -18)
    act(T1, ID, AF.Copy, scale=-2.0 ** -19)
    vtt(LQ, LS, T1, OP.add)
    act(BN, BO, AF.Copy, scale=-1.0)
    for h, v in ((G1, 1.0), (G2, 2.0 / BIG), (GM, -1.0 / BIG)):
        vts(h, sub(BO, 0, 128, 16), v, None, OP.mult)
    vset(D, 0.0)
    vcopy(sub(D, 15, 143, 16), sub(BO, 0, 128, 16))
    WF = new("af", 1)
    vcopy(WF, win_)
    vts(WD, D, WF, None, OP.mult)
    vts(WB, BO, WF, None, OP.mult)
    vset(ZERO, 0.0)

    def part(k):
        return sub(CONST, k * n, (k + 1) * n)
    for k, v in enumerate((129.0 * 4096, 65536.0 - 2.0 ** 23, 2048.0 - BIG, 113.0, 103.0)):
        vset(part(k), v)
    vset(MASK, 1.0)
    vset(sub(MASK, 0, ncol(MASK), 16), 0.0)
    B1, B2, BASE = new("ai", n // 16), new("ai", n // 16), new("ai", n // 16)
    iota(B1, [[0, n // 16]], 0, 16)
    iota(B2, [[256, n // 16]], 0, 0)
    vts(B1, B1, 255, None, OP.bitwise_and)
    vtt(BASE, B1, B2, OP.add)
    J, JF, J0 = new("ai", 1), new("af", 1), new("af", 1)
    I1, I2, PLACE = new("ai", n), new("ai", n), new("ah", n)
    F1, F2 = new("af", n), new("af", n)
    iota(J, [[0, 1]], 0, 1)
    vts(J, J, 15, None, OP.bitwise_and)
    vcopy(JF, J)
    if cfg["pad"]:
        iota(I1, [[17, n]], 1 - 1024, 0)
        vts(PLACE, I1, JF, None, OP.add)
    else:
        iota(I1, [[16, n]], n - 1024, 0)
        iota(I2, [[15, n]], n, 0)
        vts(J0, JF, 0.0, None, OP.is_equal)
        vts(F1, I1, JF, None, OP.add)
        vts(F2, I2, J0, None, OP.mult)
        vtt(PLACE, F1, F2, OP.subtract)

    big = []
    ZS = new("aw", 16 * n)
    if "V" in cfg["zx"]:
        vset(ZS, 0.0)
    for b in range(NB):
        d = {k: new("aw", SEG) for k in ("mh", "mo", "mc", "ch", "mx", "zx")}
        d["zs"] = ZS
        d["win"] = new("a3" if cfg["pad"] else "aw", 3 * SEG)
        if cfg["pad"]:
            vset(sub(d["win"], 0, 3 * SEG, 17), 255.0)
            vset(sub(d["zx"], 0, SEG, 17), 0.0)
        d.update({k: new("aw", n) for k in ("st", "rec", "want", "cnt", "am", "sv", "spl", "low", "x", "fl", "so", "fu", "g1", "g2")})
        d["ar"], d["yes"], d["p1"] = new("aw", 2 * n), new("aw", 8), new("af", 2 * n)
        d.update({k: new("ah", n) for k in ("Cc", "stK")})
        d["ABc"] = new("ah", 2 * n)
        d.update({k: new("af", n) for k in ("dhS", "m", "mw", "xg", "P", "pU", "p2", "A", "stF")})
        d.update({k: new("ai", n) for k in ("T", "C", "TU", "xf")})
        d.update({k: new("ai", n // 16) for k in ("ui", "ua", "ul")})
        d["C16"], d["ch16"], d["l16"] = new("au", n), new("au", n), new("au", n // 16)
        big.append(d)
    ACC = [new("af", 2) for _ in range(NREAD)]
    KC = [new("af", 1) for _ in range(NREAD)]
    KJ = new("af", 2)

    mail = []
    for b in range(NB):
        AB = new("au", 2 * n)
        A16, B16 = sub(AB, 0, n), sub(AB, n, 2 * n)
        vcopy(A16, sub(bain, n * b, n * b + n))
        vcopy(B16, sub(bbin, n * b, n * b + n))
        mail.append((A16, B16, sub(zin, n * b, n * b + n), ONE, None, ONE, AB))

    def after(k, d, raw, vs, dh, dc, dp, R):
        if k == "h":
            pe(vs, [(NEG, raw[j]) for j in range(8)], "voteh", stop=False)
            pe(vs, [(NEG, raw[j]) for j in range(8, 16)], "voteh", first=False, stop=False)
            copy(cfg["dhS"], d["dhS"], dh, "dhS")
        if k == "c":
            if cfg["quick"][cur[1]]:
                vtt(d["x"], d["dhS"], dc, OP.is_le, "x")
            vtt(d["m"], d["dhS"], dc, OP.min, "m")
            if cfg["quick"][cur[1]]:
                pe(dp, [(R, MID[2.0 ** -30]), (d["st"], ID), (ID, d["x"])], "pen")
                vtt(d["mw"], d["m"], dp, OP.max, "mw")
            else:
                pe(dp, [(FID[1], d["dhS"]), (R, MID[-2.0 ** -30]), (d["st"], NEG)], "pen", stop=False)

    for t in range(NREAD):
        last = t == NREAD - 1
        nxt = []
        for b in range(NB):
            cur[0], cur[1] = t, b
            d = big[b]
            Bd, Bv, Bx, By = b, 2 + b, 4 + b, 6 + b
            H16, O16, z, R = mail[b][t & 1], mail[b][1 - (t & 1)], mail[b][2], mail[b][5]
            hp, lin, zp, sel = [ps(Bx, k) for k in range(4)]
            d["Hc"], d["Oc"] = [sub(d["ABc"], k * n, k * n + n) for k in (t & 1, 1 - (t & 1))]
            vts(d["ABc"], mail[b][6], -2048.0, None, OP.add, name="Hc")
            if not cfg["pad"]:
                pe(zp, [(ID, z)], "zPS")
            pe(hp, [(HI, d["Hc"])], "HcPS")
            pe(lin, [(HID[2080], d["Hc"]), (HID[3232], d["Oc"])], "lin")
            vtt(d["P"], d["Oc"], hp, OP.mult, "P")
            vtt(d["T"], d["P"], lin, OP.add, "T")
            vts(d["C"], d["T"], 5, 4095, OP.arith_shift_right, OP.bitwise_and, name="C")
            vcopy(d["C16"], d["C"], "C16")
            vts(d["Cc"], d["C16"], -2048.0, None, OP.add, name="Cc")
            vtt(d["st"], d["Oc"], hp, OP.is_equal, "st")
            if cfg["zx"][b] == "G":
                for j in range(16):
                    copy("A" if j < cfg["zxa"][b] else "G", sub(d["zx"], j + 1, SEG, 17) if cfg["pad"] else sub(d["zx"], j, 16 * n, 16), z, "zx")
            else:
                copy(cfg["zs"], sub(d["zs"], 0, 16 * n, 16), z, "zs")
                scan(d["zx"], MASK, d["zs"], OP.mult, OP.add, "zx")
            dh, do, dc = ps(Bd, 0), ps(Bd, 1), ps(By, 2)
            vs, dp = ps(Bv, 0), ps(By, 1)
            for k, lst, dist in (("h", H16, dh), ("c", d["C16"], dc), ("o", O16, do)):
                at = SEG * "hoc".index(k)
                if cfg["pad"]:
                    col, res = sub(d["win"], at, at + SEG), d["m" + k]
                    for e, q0, q1 in pieces(cfg["col"][b][k]):
                        gath(e, sub(col, 17 * q0, 17 * q1) + ("bills",), X, sub(lst, q0, q1), name=k)
                    for _e, q0, q1 in pieces(cfg["cut"][b][k]):
                        scan(sub(res, 17 * q0, 17 * q1), sub(d["zx"], 17 * q0, 17 * q1), sub(col, 17 * q0, 17 * q1), OP.min, OP.max, "max" + k)
                    raw = [sub(col, j + 1, SEG, 17) for j in range(16)]
                    opening = (d["st"], MID[0.5 / BIG], dist) if k == "o" else (ID, ZERO, dist)
                    pe(None, [opening] + [(raw[j], GM, sub(dist, j, n, 16)) for j in range(16)], "raw" + k, stop=False)
                    pe(None, [(sub(res, j + 1, SEG, 17), G2, sub(dist, j, n, 16)) for j in range(16)], "d" + k, first=False)
                    after(k, d, raw, vs, dh, dc, dp, R)
                    continue
                side, col, res = sub(d["win"], at, at + n), sub(d["win"], at + n, at + SEG), d["m" + k]
                for e, q0, q1 in pieces(cfg["col"][b][k]):
                    gath(e, sub(col, 16 * q0, 16 * q1), X, sub(lst, q0, q1), name=k)
                for _e, q0, q1 in pieces(cfg["cut"][b][k]):
                    head = sub(col, 16 * q0, 16 * q1, 16)
                    copy(cfg["side"][b]["hco".index(k)], sub(side, q0, q1), head, "side" + k)
                    vtt(head, head, sub(zp, q0, q1), OP.max, "fix" + k)
                    scan(sub(res, 16 * q0, 16 * q1), sub(d["zx"], 16 * q0, 16 * q1), sub(col, 16 * q0, 16 * q1), OP.min, OP.max, "max" + k)
                raw = [side] + [sub(col, j, 16 * n, 16) for j in range(1, 16)]
                opening = (d["st"], MID[0.5 / BIG], dist) if k == "o" else (ID, ZERO, dist)
                for _e, q0, q1 in pieces(cfg["sum"][b][k]):
                    rows = [sub(dist, j, n, 16) + (q0, q1) for j in range(16)]
                    pe(None, [opening] * (q0 == 0) + [(sub(col, 16 * q0 + j, 16 * q1, 16), GM, rows[j]) for j in range(1, 16)], "raw" + k,
                       first=q0 == 0, stop=False)
                    pe(None, [(sub(side, q0, q1), GM, rows[0])] + [(sub(res, 16 * q0 + j, 16 * q1, 16), G2, rows[j]) for j in range(16)],
                       "d" + k, first=False, stop=q1 == n)
                after(k, d, raw, vs, dh, dc, dp, R)
            cap = ps(By, 0)
            if cfg["quick"][b]:
                vtt(d["want"], d["mw"], do, OP.is_lt, "want")
                vtt(d["rec"], d["m"], do, OP.is_ge, "rec")
            else:
                vtt(d["rec"], d["m"], do, OP.is_ge, "rec")
                pe(dp, [(NEG, d["rec"])], "penr", first=False)
                vtt(d["want"], d["m"], dp, OP.is_lt, "want")
            scan(d["cnt"], sub(MASK, 0, n), d["want"], OP.mult, OP.add, "cntw")
            pe(sel, [(HI, PLACE), (d["rec"], MID[SEG])], "sel", stop=False)
            pe(cap, [(d["want"], MID[-64]), (d["cnt"], ID)], "cap")
            act(d["am"], cap, AF.Sign, scale=-1.0, bias=-59.5, name="am")
            pe(sel, [(MID[SEG], d["am"])], "sel2", first=False)
            vts(d["ch16"], sel, 1024.0 + SEG, None, OP.add, name="ch16")
            for e, q0, q1 in pieces(cfg["ch"][b]):
                gath(e, sub(d["ch"], 16 * q0, 16 * q1), d["win"], sub(d["ch16"], q0, q1), name="ch")
                scan(sub(d["mx"], 16 * q0, 16 * q1), sub(MASK, 0, 16 * (q1 - q0)), sub(d["ch"], 16 * q0, 16 * q1), OP.mult, OP.max, "mx")
            for q0 in (0, n // 2):
                pe(sub(vs, q0, q0 + n // 2), [(ID, sub(d["ch"], 16 * q0 + j, 16 * q0 + 8 * n, 16)) for j in range(16)], "vote", first=False, stop=q0 > 0)
        for b in range(NB):
            cur[0], cur[1] = t, b
            d = big[b]
            Bd, Bv, Bx, By = b, 2 + b, 4 + b, 6 + b
            M = sub(d["mx"], 15, 16 * n, 16)
            out = {}
            if not last:
                out["AB"] = new("au", 2 * n)
                out["ZIG"] = new("aw", 4 * n)
                out["A"], out["B"] = sub(out["AB"], 0, n), sub(out["AB"], n, 2 * n)
                out["z"], out["I"], out["S"], out["G"] = [sub(out["ZIG"], k * n, (k + 1) * n) for k in range(4)]
                ulp = ps(Bx, 3, n // 16)
                pe(ulp, [(sub(WD, 15 - j, 143 - j), sub(d["mx"], 15 + 16 * j, 16 * n, 256)) for j in range(16)], "ulist")
                vcopy(d["ui"], ulp, "ui")
                vts(d["ua"], d["ui"], 15, None, OP.bitwise_and, name="ua")
                vtt(d["ul"], d["ua"], BASE, OP.add, "ul")
                vcopy(d["l16"], d["ul"], "l16")
                xw = sub(X, 16 * n * b, 16 * n * (b + 1))
                if cfg["xg"][b] == "V":
                    gath("V", d["xg"], xw, d["l16"], M, OP.add, "xg")
                    vts(d["xf"], d["xg"], -0.5, 0.5, OP.add, OP.mult, name="xf")
                else:
                    pe(ps(Bx, 0), [(MID[0.5], M)], "Mh")
                    add("A", 0.065 + CY * GR * n, [xw, d["l16"]], [d["xg"]],
                        lambda q, V, d=d, xw=xw: q.activation(V(d["xg"]), V(xw).indirect(V(d["l16"])), AF.Copy, -0.25, 0.5), "xg")
                    vtt(d["xf"], d["xg"], ps(Bx, 0), OP.add, "xf")
                add("V", 0.05 + CY * 3.8 * n, [d["xf"], d["l16"]], [xw],
                    lambda q, V, d=d, xw=xw: q.tensor_copy(V(xw).indirect(V(d["l16"])), V(d["xf"])), "scat")
            else:
                out["A"], out["B"], out["I"], out["G"] = [new("af", n) for _ in range(4)]
            d["out"] = out
        for b in range(NB):
            cur[0], cur[1] = t, b
            d = big[b]
            Bd, Bv, Bx, By = b, 2 + b, 4 + b, 6 + b
            z, low0, spl0, R = mail[b][2:6]
            out, M = d["out"], sub(d["mx"], 15, 16 * n, 16)
            Hc, Oc, Cc, st = d["Hc"], d["Oc"], d["Cc"], d["st"]
            ay, ry = sub(d["ar"], 0, n), sub(d["ar"], n, 2 * n)
            Bt, Lt, DC, DO = [ps(Bd, k) for k in range(4)]
            ur, zd, Ht = ps(Bx, 1), ps(Bx, 2), ps(Bx, 3)
            vs, ct, y, par = ps(Bv, 0), ps(Bv, 1, 8), ps(Bv, 2), ps(Bv, 3)
            Rt, At, st_ = ps(By, 0), ps(By, 2), ps(By, 3)
            pe(DC, [(HI, Cc), (HID[-1], Hc)], "DC")
            pe(DO, [(HI, Oc), (HID[-1], Hc)], "DO")
            pe(At, [(ID, part(2)), (HI, Hc), (MID[BIG], st)], "At")
            spl, low = (d["spl"], d["low"]) if last else (out["S"], out["I"])
            pe(st_, [(MID[-64], low0), (MID[-128], st), (d["rec"], MID[-64]), (MID[-32], d["am"])]
               + ([(MID[-2.0 ** -10], spl0)] if t > 0 else []), "splt", stop=False)
            act(d["sv"], vs, AF.Sign, bias=0.5, name="sv")
            pe(st_, [(BN, d["sv"])], "splt", first=False)
            vts(spl, st_, 33.0, 2.0 ** 17, OP.is_gt, OP.mult, name="spl")
            act(low, st_, AF.Sign, scale=-1.0, bias=-94.5, name="low")
            pe(None, [(BO, d["sv"], ps(By, 0)), (MID[32], d["am"], ps(By, 0))], "ayt")
            pe(None, [(BO, d["sv"], ps(By, 1)), (d["rec"], MID[32], ps(By, 1))], "ryt")
            act(d["ar"], ps(By, 0, 2 * n), AF.Sign, bias=-31.0, name="ar")
            more = []
            if t > 0 and cfg["stK"] == "V":
                vts(d["stK"], st, KC[t - 1], None, OP.mult, name="stK")
                more = [(HID[32], d["stK"], Lt)]
            elif t > 0:
                add("A", AO + CY * n, [st, KC[t - 1]], [d["stF"]],
                    lambda q, V, d=d, k=KC[t - 1]: q.activation(V(d["stF"]), V(d["st"]), AF.Copy, 0.0, V(k)), "stK")
                more = [(FID[32], d["stF"], Lt)]
            pe(None, [(ID, sub(CONST, 0, 2 * n), ps(Bd, 0, 2 * n)), (HID[32], Oc, Lt)] + more, "g2", stop=False)
            pe(ur, [(WB, M)], "uraw")
            act(d["fu"], ur, AF.Copy, scale=1.0 / 4096, bias=128.5 + 1.0 / 8192, name="fu")
            pe(Bt, [(MID[-4096], d["fu"]), (WB, M), (HID[-2.0 ** -12], Oc), (HID[2.0 ** -12], Hc)], "u", first=False, stop=False)
            if not last:
                pe(zd, [(ID, z), (NEG, M)], "zd")
                act(out["z"], zd, AF.Abs, name="z")
                pe(ct, [(d["sv"], G1)], "ct")
                act(d["yes"], ct, AF.Sign, bias=0.5, acc=sub(ACC[t], b, b + 1), name="yes")
                if b == NB - 1:
                    kt = ps(Bv, 1, NB)
                    pe(kt, [(HALF, ACC[t])], "kt")
                    act(KJ, kt, AF.Copy, bias=4.0 * n, acc=KC[t], name="K")
            pe(par, [(MID[1.25], part(4)), (LQ, spl)], "par")
            vtt(d["p1"], d["ar"], ps(Bd, 2, 2 * n), OP.mult, "p1")
            pe(Ht, [(HID[0.5], Cc), (HID[0.5], Oc), (FID[0.5], sub(d["p1"], 0, n)), (FID[0.5], sub(d["p1"], n, 2 * n))], "H1", stop=False)
            if not last:
                pe(Rt, [(MID[145], part(3)), (MID[2 * BIG], ay)], "Rt")
                vtt(out["G"], R, Rt, OP.mult, "G")
                zl, la = new("aw", 4 * n), new("au", 2 * n)
                if cfg["zmail"][b]:
                    mailto(out["z"], sub(zl, 0, n), "rq", t, b)
                    mailto(sub(out["ZIG"], n, 4 * n), sub(zl, n, 4 * n), "rz", t, b)
                else:
                    mailto(out["ZIG"], zl, "rz", t, b)
            else:
                pe(y, [(MID[-0.5], low), (MID[-2.0 ** -17], spl)], "y")
                act(out["I"], y, AF.Copy, bias=0.5, name="I")
                vts(d["g1"], R, 2.0, None, OP.is_ge, name="once")
                vts(d["g2"], R, 2.0 ** 20, None, OP.is_ge, name="twice")
                pe(Rt, [(ID, d["g1"]), (ID, d["g2"]), (MID[0.5], ay)], "Rt")
                act(out["G"], Rt, AF.Copy, bias=0.5, name="G")
            vtt(d["A"], spl, At, OP.max, "A")
            copy(cfg["fl"][b], d["fl"], par, "fl")
            vtt(d["so"], d["fl"], par, OP.is_equal, "so")
            vtt(d["p2"], d["so"], DC, OP.mult, "p2")
            pe(Bt, [(FID[2.0 ** -12], d["p2"])], "B2", first=False)
            pe(Ht, [(FID[1], d["p2"])], "H2", first=False)
            oh, oo = (out["A"], out["B"]) if t % 2 == 0 else (out["B"], out["A"])
            vtt(d["pU"], d["A"], Bt, OP.mult, "pU")
            vtt(d["TU"], d["pU"], Lt, OP.add, "TU")
            vts(oh, Ht, 2048.0, None, OP.add, name="nH")
            la_h, la_o = [sub(la, k * n, k * n + n) for k in ((0, 1) if t % 2 == 0 else (1, 0))] if not last else (None, None)
            if not last and cfg["mails"] == 3:
                mailto(oh, la_h, "rh", t, b)
            vts(d["TU"], d["TU"], 5, 4095, OP.arith_shift_right, OP.bitwise_and, name="U")
            vcopy(oo, d["TU"], "nO")
            if not last:
                if cfg["mails"] == 3:
                    mailto(oo, la_o, "ro", t, b)
                else:
                    mailto(out["AB"], la, "ro", t, b)
                nxt.append((sub(la, 0, n), sub(la, n, 2 * n)) + tuple(sub(zl, k * n, k * n + n) for k in range(4)) + (la,))
            else:
                for k, nme in (("G", "yg"), ("I", "yi"), ("A", "ya"), ("B", "yb")):
                    add("S", 0.1, [out[k]], [], lambda q, V, nme=nme, h=out[k], a=n * b: q.dma_start(V(nme)[:, a:a + n], V(h)), "st" + nme, "dma", "st%s%d" % (nme, b))
        mail = nxt
    return ops


def depend(ops):
    hist = {}
    closed, since = {}, {}
    for i, o in enumerate(ops):
        dep = set(o["x"])
        for h, w in [(h, 0) for h in o["r"]] + [(h, 1) for h in o["w"]]:
            for j, a, b, jw, s in hist.get(h[0], ()):
                if (w or jw) and a < h[2] and h[1] < b and not (s == h[3] > 1 and (a - h[1]) % s):
                    dep.add(j)
        for h, w in [(h, 0) for h in o["r"]] + [(h, 1) for h in o["w"]]:
            lst = hist.setdefault(h[0], [])
            if w:
                lst[:] = [e for e in lst if not (h[1] <= e[1] and e[2] <= h[2] and (h[3] == 1 or (h[3] == e[4] and (e[1] - h[1]) % h[3] == 0)))]
            lst.append((i, h[1], h[2], w, h[3]))
        if o["g"]:
            bank, first, stop = o["g"]
            if first and bank in closed:
                dep.add(closed[bank])
            if first != stop or not first:
                if first or stop:
                    dep.update(since.get(bank, ()))
                    since[bank] = []
                if stop:
                    closed[bank] = i
            since.setdefault(bank, []).append(i)
        dep.discard(i)
        o["d"] = sorted(dep)
        o["b"] = sorted({h[0] for h in o["r"] + o["w"] if h[0] not in DTY})


LDT = {"ldba": 3.0, "ldbb": 3.2, "ldzp": 3.4, "ldwl": 3.4, "ldxt": 7.0}


GATHERS = ("h", "o", "c", "ch", "xg")


def costs(ops, f, gr, net, send):
    hold, fin = [], []
    for o in ops:
        x = o["c"]
        if o["k"] == "net":
            x = net
        elif o["k"] == "send":
            x = send
        elif o["k"] == "c":
            x = f * (0.06 + (x - 0.06) * gr / GR if o["n"] in GATHERS else x)
        hold.append(x)
        fin.append(LDT.get(o["n"], 2.5) if o["k"] == "dma" else x)
    return hold, fin


def times(order, eng, pred, banks, hold, fin, wake):
    m = len(order)
    start, end, why, soft = [0.0] * m, [0.0] * m, [-1] * m, [False] * m
    free = {e: (0.0, -1) for e in "VAPGSN"}
    used = [{} for _ in range(8)]
    for i in order:
        e = eng[i]
        t, w = free[e]
        sf = True
        for j, same in pred[i]:
            u = end[j] + (SAME if same else wake)
            if u > t:
                t, w, sf = u, j, False
        for b in banks[i]:
            for e2, (u, j) in used[b].items():
                if e2 != e and u + wake > t:
                    t, w, sf = u + wake, j, True
        why[i], soft[i], start[i], end[i] = w, sf, t, t + fin[i]
        if e != "N":
            free[e] = (t + hold[i], i)
        for b in banks[i]:
            used[b][e] = (end[i], i)
    i = end.index(max(end))
    pairs = []
    while why[i] >= 0:
        if soft[i]:
            pairs.append((why[i], i))
        i = why[i]
    return start, end, pairs


def plan(ops, turn):
    words = turn.split()
    place = {w.rstrip("+-"): k + len(words) * ((w[-1] == "+") - (w[-1] == "-")) for k, w in enumerate(words)}
    seen, want, loaded = {}, [], []
    for o in ops:
        k = (o["n"], o["blk"], o["t"], o["k"])
        seen[k] = seen.get(k, 0) + 1
        name = "%s%d%s" % (o["n"], o["blk"], " bcdefghijklmnop"[min(seen[k], 16) - 1].strip())
        want.append(place[name] + len(words) * o["t"] if name in place and o["k"] != "net" and o["t"] >= 0 else None)
        if o["t"] == 0 and name in EARLY:
            want[-1] -= 5e5
        loaded.append(o["k"] == "dma" or any(loaded[j] for j in o["d"]))
    need = [w if w is not None else 1e5 for w in want]
    for i in range(len(ops) - 1, -1, -1):
        for j in ops[i]["d"]:
            need[j] = min(need[j], need[i])
    key = []
    for i, o in enumerate(ops):
        k = want[i]
        if k is None:
            if o["t"] >= 0 or o["k"] == "dma":
                k = -2e6
            elif loaded[i]:
                k = need[i] - 0.5
            else:
                k = need[i] - (1e6 if need[i] <= place[SOON] else 1e5)
        key.append(max([k] + [key[j] + 1e-6 for j in o["d"]]))
    return sorted(range(len(ops)), key=lambda i: key[i])


OPS = build(CFG)
depend(OPS)
ORDER = plan(OPS, TURN)
PLACE_OF = {i: k for k, i in enumerate(ORDER)}

SCRATCH = {k: ("sbuf", [128, _size[k] // 17, 17] if k == "a3" else [128, _size[k]], DTY[k][0]) for k in DTY if _size[k]}
SCRATCH.update({"ps%d" % k: ("psum", [128, 512], "float32") for k in range(8)})
SEMAPHORES = ["cV", "cA", "cP", "cG", "sent"] + sorted({o["s"] for o in OPS if o["s"]})


def rank_program(g, core, T, topo):
    rank = T.rank_of(core)
    if rank is None:
        return
    dst = T.cores[(rank + 1) % len(T.cores)]
    rid, pid, _ = topo.addr(dst)
    mask = topo.mask(core, dst)
    width = len(topo.engines(core, dst))
    queue = {"V": g.vector, "A": g.scalar, "P": g.tensor, "G": g, "S": g.sync}

    def V(h):
        return view(T, h)

    count = {e: 0 for e in "VAPG"}
    know = {e: {} for e in queue}
    snap = {}
    lastb = {}
    sent = 0
    sig = {}

    def need(e, i):
        s, c = sig[i]
        if know[e].get(s, 0) >= c:
            return
        queue[e].wait_ge(T.sem[s], c)
        for k, v in snap[i].items():
            if know[e].get(k, 0) < v:
                know[e][k] = v
        know[e][s] = c

    for i in ORDER:
        o = OPS[i]
        e = o["e"]
        if o["k"] == "net":
            sig[i] = (o["s"], width)
            snap[i] = {}
            continue
        deps = {j for j in o["d"] if OPS[j]["k"] != "send" and e + OPS[j]["e"] != "PP"}
        for b in o["b"]:
            for e2, j in lastb.get(b, {}).items():
                if e2 != e:
                    deps.add(j)
        for j in sorted(deps, key=lambda j: -PLACE_OF[j]):
            need(e, j)
        if o["k"] == "send":
            _s, src, land, sem = o["f"]
            g.remote_dma(V(land), V(src), T.sem[sem], T.sem.sent, pid, rid, mask)
            sent += width
            continue
        ins = o["f"](queue[e], V)
        if o["k"] == "dma":
            ins.then_inc(T.sem[o["s"]], 16)
            sig[i] = (o["s"], 16)
            snap[i] = dict(know[e])
        else:
            count[e] += 1
            ins.then_inc(T.sem["c" + e], 1)
            sig[i] = ("c" + e, count[e])
            snap[i] = dict(know[e])
            for b in o["b"]:
                lastb.setdefault(b, {})[e] = i
    for e in "VAPG":
        g.wait_ge(T.sem["c" + e], count[e])
    for i in ORDER:
        if OPS[i]["k"] in ("dma", "net"):
            g.wait_ge(T.sem[OPS[i]["s"]], sig[i][1])
    g.wait_ge(T.sem.sent, sent)
